import numpy as np
import ml_dtypes


def mxq(x, axis, fmt="e4m3"):
    dtype, down = {"e4m3": (ml_dtypes.float8_e4m3fn, 7), "e5m2": (ml_dtypes.float8_e5m2, 14)}[fmt]
    v = np.moveaxis(np.asarray(x, np.float32).astype(ml_dtypes.bfloat16).astype(np.float64), axis, -1)
    blocks = v.reshape(v.shape[:-1] + (-1, 32))
    amax = np.abs(blocks).max(-1, keepdims=True)
    byte = np.maximum(np.where(amax > 0, np.frexp(amax)[1] - 1 + 127, 0) - down, 1)
    scale = np.exp2(byte - 127.0)
    codes = (blocks / scale).astype(np.float32).astype(dtype).astype(np.float64)
    return np.moveaxis((codes * scale).reshape(v.shape), -1, axis)


WIDE = False


def mx_kscale(k):
    if not WIDE:
        return np.ones(k)
    levels = np.array([10, -10, 5, -5, 0])
    if k % 512:
        return np.exp2(np.random.permutation(np.resize(levels, k // 32))).repeat(32)
    a = np.empty((k // 512, 16))
    for p in range(k // 512):
        a[p, :8] = np.random.permutation(np.resize(levels, 8))
        for g in range(8):
            far = levels[np.abs(levels - a[p, g]) >= 10]
            a[p, g + 8] = far[np.random.randint(len(far))]
    return np.exp2(a.ravel()).repeat(32)


BF16 = ml_dtypes.bfloat16


def bf(x):
    return np.asarray(x, np.float32).astype(BF16)


def f64(x):
    return np.asarray(x).astype(np.float64)


E2M1 = np.array([0.0, 0.5, 1.0, 1.5, 2.0, 3.0, 4.0, 6.0, -0.0, -0.5, -1.0, -1.5, -2.0, -3.0, -4.0, -6.0])


def pack_weight(w, fmt):
    k, n = w.shape
    w = f64(bf(w)).reshape(k // 32, 32, n)
    amax = np.abs(w).max(1)
    if fmt == "e4m3":
        byte = np.frexp(amax)[1] - 1 + 127 - 7
    else:
        mant, ex = np.frexp(amax / 6.0)
        byte = np.where(mant > 0.5, ex, ex - 1) + 127
    byte = np.clip(np.where(amax > 0, byte, 1), 1, 254)
    scaled = (w * np.exp2(127.0 - byte)[:, None, :]).reshape(k, n).astype(np.float32)
    by_word = np.ascontiguousarray(scaled.reshape(k // 512, 128, 4, n).transpose(0, 1, 3, 2))
    if fmt == "e4m3":
        words = by_word.astype(ml_dtypes.float8_e4m3fn).view(np.uint8)
    else:
        c = by_word.astype(ml_dtypes.float4_e2m1fn).view(np.uint8) & 0xF
        words = c[..., 0::2] | (c[..., 1::2] << 4)
    return np.ascontiguousarray(words), np.ascontiguousarray(byte.astype(np.uint8).reshape(k // 512, 16, n))


def unpack_weight(words, scales, fmt):
    g, p, n, _ = words.shape
    if fmt == "e4m3":
        vals = np.ascontiguousarray(words).view(ml_dtypes.float8_e4m3fn).astype(np.float64)
    else:
        nib = np.empty((g, p, n, 4), np.uint8)
        nib[..., 0::2] = words & 0xF
        nib[..., 1::2] = words >> 4
        vals = E2M1[nib]
    vals = vals * np.repeat(np.exp2(scales.astype(np.float64) - 127.0), 8, axis=1)[..., None]
    return vals.transpose(0, 1, 3, 2).reshape(g * 512, n)
def pack4(w):
    words, scales = pack_weight(w, "e2m1")
    return words.reshape(words.shape[0], 128, -1), scales


def unpack4(words, scales):
    return unpack_weight(words.reshape(words.shape[0], 128, -1, 2), scales, "e2m1")


def planes(Y):
    n, m = Y.shape
    b = f64(bf(Y)).reshape(n // 32, 32, m)
    amax = np.abs(b).max(1)
    byte = np.clip(np.where(amax > 0, np.frexp(amax)[1] - 1 + 127 - 7, 1), 1, 254)
    codes = (b * np.exp2(127.0 - byte)[:, None, :]).reshape(n, m).astype(np.float32).astype(ml_dtypes.float8_e4m3fn).view(np.uint8)
    words = codes.reshape(n // 512, 128, 4, m).transpose(0, 1, 3, 2)
    return np.ascontiguousarray(words), np.ascontiguousarray(byte.astype(np.uint8).reshape(n // 512, 16, m))


B, T, U, KE, KP, J = 64, 16, 4, 2048, 1024, 1024

def setup_inputs():
    s = mx_kscale(KE)
    r = mx_kscale(KP)
    enc = np.random.randn(B, T, KE) * s
    we = 0.7 * np.random.randn(KE, J) / np.sqrt(KE) / s[:, None]
    pred = np.random.randn(B, U, KP) * r
    wp = 0.7 * np.random.randn(KP, J) / np.sqrt(KP) / r[:, None]
    bias = 0.3 * np.random.randn(J)
    gain = np.exp(0.8 * np.random.randn(J))
    we_words, we_scales = pack4(we)
    return {"enc": bf(enc), "we_words": we_words, "we_scales": we_scales,
            "pred": bf(pred), "wp": bf(wp), "bias": bf(bias), "gain": bf(gain)}

def reference(enc, we_words, we_scales, pred, wp, bias, gain):
    xe = mxq(f64(enc).reshape(B * T, KE), 1, "e4m3")
    e = xe @ unpack4(we_words, we_scales)
    xp = mxq(f64(pred).reshape(B * U, KP), 1, "e4m3")
    p = xp @ mxq(f64(wp), 0, "e4m3")
    z = e.reshape(B, T, 1, J) + p.reshape(B, 1, U, J) + f64(bias)
    y = np.tanh(z) * f64(gain)
    Y = y.reshape(B * T * U, J).T
    words, scales = planes(Y)
    return y, words, scales

@@ -1,0 +1,415 @@
+from contextlib import ExitStack
+
+import concourse.mybir as mybir
+from concourse.masks import make_identity
+
+B, T, U, KE, KP, J = 64, 16, 4, 2048, 1024, 1024
+FLOPS = 2 * B * T * KE * J + 2 * B * U * KP * J
+
+F32 = mybir.dt.float32
+BF16 = mybir.dt.bfloat16
+I32 = mybir.dt.int32
+U32 = mybir.dt.uint32
+U8 = mybir.dt.uint8
+FP8X4 = mybir.dt.float8_e4m3fn_x4
+FP4X4 = mybir.dt.float4_e2m1fn_x4
+ACT = mybir.ActivationFunctionType
+ALU = mybir.AluOpType
+
+P = 128
+HALF = 512
+CE = KE // 512
+CP = KP // 512
+NB = HALF // P
+
+VECTOR_ADD_F0 = (1, 3)
+CAST_ON_GPSIMD = True
+Z_BANKS, W_BANKS, M_BANKS = 3, 1, 3
+SHARED = True
+WA, WB = 2, 3
+YB = 4
+TAIL_V = 2
+WP_S = 128
+QP = 2
+P_K = 1
+WPK = 3
+QK = 3
+SH = 0
+P4B = 8
+ENC_EVAC_V = 0
+
+
+def tile_transducer_joint_hidden_planes_g5_kernel(
+    tc, enc, we_words, we_scales, pred, wp, bias, gain, out_0, out_1, out_2
+):
+    nc = tc.nc
+    enc_rows = enc.rearrange("(h i) (fh f0) k -> h f0 (i fh) k", h=2, f0=4)
+    pred_rows = pred.rearrange("(h i) u k -> h (i u) k", h=2)
+    y_rows = out_0.rearrange("(h i) (fh f0) u j -> h f0 (i fh) u j", h=2, f0=4)
+    words_out = out_1.rearrange("g p m t -> g p (m t)").bitcast(I32)
+
+    groups = [(0, 0), (1, 0), (0, 1), (1, 1)]
+    pairs = [
+        (h, g, 2 * a + odd, up)
+        for (h, g) in groups
+        for a in range(2)
+        for up in range(2)
+        for odd in range(2)
+    ]
+    n_pairs = len(pairs)
+
+    with ExitStack() as ctx:
+        keep = ctx.enter_context(tc.tile_pool(name="keep", bufs=1))
+        work = ctx.enter_context(tc.tile_pool(name="work", bufs=2))
+        psum = ctx.enter_context(tc.psum_pool(name="psum", bufs=1))
+        ctx.enter_context(tc.manual_schedule())
+
+        def bank(tag, bufs):
+            if SHARED and tag != "gain":
+                return psum.tile([P, HALF], F32, name="ring", tag="ring", bufs=7)
+            return psum.tile([P, HALF], F32, name=tag, tag=tag, bufs=bufs)
+
+        def misc_bank():
+            return bank("misc", M_BANKS)
+
+        ident = keep.tile([P, P], F32, name="ident")
+        bg_rows = keep.tile([P, P], BF16, name="bg_rows")
+        we_plane = keep.tile([P, CE * J], U8, name="we_plane", align_bytes=64)
+        nc.vector.memset(bg_rows[:], 0.0)
+        nc.vector.memset(we_plane[:].bitcast(I32), 0)
+        make_identity(nc, ident[:])
+        warm = keep.tile([P, 1], F32, name="warm")
+        nc.scalar.activation(out=warm[:], in_=bg_rows[:, 0:1], func=ACT.Tanh)
+
+        wp_raw, we_codes, enc_raw, pred_raw = {}, {}, {}, {}
+
+        def load_wp(g, c):
+            wp_raw[g, c] = keep.tile([P, 4, HALF], BF16, name="wp_raw%d%d" % (g, c), align_bytes=64)
+            src = wp[512 * c : 512 * (c + 1), HALF * g : HALF * (g + 1)]
+            nc.sync.dma_start(out=wp_raw[g, c][:], in_=src.rearrange("(p t) n -> p t n", t=4))
+
+        def load_we(g):
+            we_codes[g] = keep.tile([P, CE, 2 * HALF], U8, name="we_codes%d" % g, align_bytes=64)
+            src = we_words[:, :, 2 * HALF * g : 2 * HALF * (g + 1)].rearrange("c p n -> p c n")
+            nc.sync.dma_start(out=we_codes[g][:].bitcast(I32), in_=src.bitcast(I32))
+
+        def load_enc(h, f0):
+            enc_raw[h, f0] = keep.tile([P, KE], BF16, name="enc_raw%d%d" % (h, f0), align_bytes=64)
+            nc.sync.dma_start(out=enc_raw[h, f0][:], in_=enc_rows[h, f0])
+
+        def load_pred(h):
+            pred_raw[h] = keep.tile([P, KP], BF16, name="pred_raw%d" % h, align_bytes=64)
+            nc.sync.dma_start(out=pred_raw[h][:], in_=pred_rows[h])
+
+        load_wp(0, 0)
+        load_enc(0, 0)
+        load_wp(0, 1)
+        load_pred(0)
+        load_we(0)
+        plane3 = we_plane[:].rearrange("p (c n) -> p c n", c=CE)
+        for quad in range(4):
+            src = we_scales[:, 4 * quad : 4 * quad + 4, :].rearrange("c r n -> r c n")
+            nc.sync.dma_start(out=plane3[32 * quad : 32 * quad + 4].bitcast(I32), in_=src.bitcast(I32))
+        nc.sync.dma_start(out=bg_rows[0:8, :], in_=bias.rearrange("(c p) -> c p", p=P))
+        nc.sync.dma_start(out=bg_rows[8:16, :], in_=gain.rearrange("(c p) -> c p", p=P))
+        for f0 in ((1, 2, 3) if SH else (1, 3, 2)):
+            load_enc(0, f0)
+        load_pred(1)
+        for f0 in ((0, 1, 2, 3) if SH else (1, 0, 3, 2)):
+            load_enc(1, f0)
+        load_wp(1, 0)
+        load_wp(1, 1)
+        load_we(1)
+
+        bg_cols = keep.tile([P, 16], F32, name="bg_cols")
+
+        def turn_bias_gain():
+            bg32 = keep.tile([P, P], F32, name="bg32")
+            nc.vector.tensor_copy(out=bg32[:], in_=bg_rows[:])
+            bg_ps = misc_bank()
+            nc.tensor.transpose(bg_ps[:, 0:P], bg32[:], ident[:])
+            nc.scalar.copy(out=bg_cols[:], in_=bg_ps[:, 0:16])
+
+        gain_ps = {}
+
+        def spread_gain(g):
+            gain_ps[g] = bank("gain", 1)
+            for jb in range(NB):
+                col = 8 + NB * g + jb
+                nc.tensor.transpose(
+                    gain_ps[g][:, P * jb : P * (jb + 1)], bg_cols[:, col : col + 1].to_broadcast([P, P]), ident[:]
+                )
+
+        def copy_out(on_vector, out, in_):
+            if on_vector:
+                nc.vector.tensor_copy(out=out, in_=in_)
+            else:
+                nc.scalar.copy(out=out, in_=in_)
+
+        wp_codes, wp_plane = {}, {}
+
+        def quantize_wp(g, c, scalar_cols=0):
+            grouped = work.tile([P, HALF * 4], BF16, name="wp_grouped", align_bytes=64)
+            dst = grouped[:].rearrange("p (n i t) -> p n t i", i=4, t=4)
+            src = wp_raw[g, c][:].rearrange("p t (n i) -> p n t i", i=4)
+            cut = (HALF - scalar_cols) // 4
+            nc.vector.tensor_copy(out=dst[:, :cut], in_=src[:, :cut])
+            if scalar_cols:
+                nc.scalar.copy(out=dst[:, cut:], in_=src[:, cut:])
+            wp_codes[g, c] = keep.tile([P, HALF], U32, name="wp_codes%d%d" % (g, c), align_bytes=64)
+            wp_plane[g, c] = keep.tile([P, HALF], U8, name="wp_plane%d%d" % (g, c), align_bytes=64)
+            return grouped
+
+        def finish_wp(g, c, grouped):
+            nc.vector.quantize_mx(out=wp_codes[g, c][:].bitcast(FP8X4), scales=wp_plane[g, c][:], in_=grouped[:])
+
+        act_grouped, act_codes, act_plane = {}, {}, {}
+
+        def turn_rows(key, raw, passes, on_vector=0):
+            words = raw[:].bitcast(F32)
+            act_grouped[key] = work.tile([P, passes * 2 * P], F32, name="act_grouped", align_bytes=64, bufs=3)
+            for c2 in range(passes // 2):
+                ps = misc_bank()
+                for cc in range(2):
+                    c = 2 * c2 + cc
+                    for hh in range(2):
+                        blk = 2 * cc + hh
+                        nc.tensor.transpose(
+                            ps[:, P * blk : P * (blk + 1)], words[:, 256 * c + hh : 256 * (c + 1) : 2], ident[:]
+                        )
+                copy_out(
+                    c2 < on_vector,
+                    act_grouped[key][:, HALF * c2 : HALF * (c2 + 1)].rearrange("p (c q hh) -> p c q hh", c=2, hh=2),
+                    ps[:].rearrange("p (c hh q) -> p c q hh", c=2, hh=2),
+                )
+
+        def quantize_rows(key, passes):
+            name = "act%s%d%d" % key
+            act_codes[key] = keep.tile([P, passes * P], U32, name=name + "c", align_bytes=64)
+            act_plane[key] = keep.tile([P, passes * P], U8, name=name + "s", align_bytes=64)
+            nc.vector.quantize_mx(
+                out=act_codes[key][:].bitcast(FP8X4), scales=act_plane[key][:], in_=act_grouped[key][:].bitcast(BF16)
+            )
+
+        e_sb, p4 = {}, {}
+
+        def make_e(h, g, f0):
+            codes, plane = act_codes["e", h, f0], act_plane["e", h, f0]
+            ps = misc_bank()
+            if f0 in VECTOR_ADD_F0:
+                for c in range(CE):
+                    nc.tensor.matmul_mx(
+                        out=ps[:],
+                        lhsT=codes[:, P * c : P * (c + 1)].bitcast(FP8X4),
+                        lhsT_scale=plane[:, P * c : P * (c + 1)],
+                        rhs=we_codes[g][:, c, :].bitcast(FP4X4),
+                        rhs_scale=we_plane[:, J * c + HALF * g : J * c + HALF * (g + 1)],
+                        start=(c == 0),
+                        stop=(c == CE - 1),
+                    )
+            else:
+                for jb in range(NB):
+                    for c in range(CE):
+                        j0 = J * c + HALF * g + P * jb
+                        nc.tensor.matmul_mx(
+                            out=ps[:, P * jb : P * (jb + 1)],
+                            lhsT=we_codes[g][:, c, 2 * P * jb : 2 * P * (jb + 1)].bitcast(FP4X4),
+                            lhsT_scale=we_plane[:, j0 : j0 + P],
+                            rhs=codes[:, P * c : P * (c + 1)].bitcast(FP8X4),
+                            rhs_scale=plane[:, P * c : P * (c + 1)],
+                            start=(c == 0),
+                            stop=(c == CE - 1),
+                        )
+            e_sb[h, g, f0] = work.tile([P, HALF], F32, name="e_sb", bufs=4)
+            nc.scalar.copy(out=e_sb[h, g, f0][:], in_=ps[:])
+
+        def make_p(h, g, blocks):
+            codes, plane = act_codes["p", h, 0], act_plane["p", h, 0]
+            ps = misc_bank()
+            for jb in blocks:
+                for c in range(CP):
+                    nc.tensor.matmul_mx(
+                        out=ps[:, P * jb : P * (jb + 1)],
+                        lhsT=wp_codes[g, c][:, P * jb : P * (jb + 1)].bitcast(FP8X4),
+                        lhsT_scale=wp_plane[g, c][:, P * jb : P * (jb + 1)],
+                        rhs=codes[:, P * c : P * (c + 1)].bitcast(FP8X4),
+                        rhs_scale=plane[:, P * c : P * (c + 1)],
+                        start=(c == 0),
+                        stop=(c == CP - 1),
+                    )
+            return ps
+
+        def spread_p_by_state(h, g, u, ps):
+            tile = work.tile([P, NB, 32, 4], F32, name="p4", bufs=P4B)
+            src = ps[:].rearrange("p (jb i u) -> p jb i u", jb=NB, u=U)[:, :, :, u : u + 1]
+            cols = bg_cols[:, NB * g : NB * (g + 1)].unsqueeze(2).unsqueeze(3)
+            nc.vector.tensor_tensor(
+                out=tile[:], in0=src.to_broadcast([P, NB, 32, 4]), in1=cols.to_broadcast([P, NB, 32, 4]), op=ALU.add
+            )
+            for jb in range(NB):
+                p4[h, g, jb, u] = tile[:, jb].rearrange("p i fh -> p (i fh)")
+
+        def spread_p_by_block(h, g, jb, ps):
+            tile = work.tile([P, U, 32, 4], F32, name="p4", bufs=P4B)
+            src = ps[:, P * jb : P * (jb + 1)].rearrange("p (i u) -> p u i", u=U).unsqueeze(3)
+            col = bg_cols[:, NB * g + jb : NB * g + jb + 1]
+            nc.scalar.activation(out=tile[:], in_=src.to_broadcast([P, U, 32, 4]), func=ACT.Identity, bias=col)
+            for u in range(U):
+                p4[h, g, jb, u] = tile[:, u].rearrange("p i fh -> p (i fh)")
+
+        z_ps, z_sb, t_sb, y_sb, y_bf, y_grouped = {}, {}, {}, {}, {}, {}
+
+        def sum_z(n):
+            h, g, f0, up = pairs[n]
+            on_vector = f0 in VECTOR_ADD_F0
+            if on_vector:
+                z_sb[n] = work.tile([P, 2, HALF], F32, name="z_sb")
+            else:
+                t_sb[n] = work.tile([P, 2, HALF], F32, name="t_sb", bufs=4)
+            for uu in range(2):
+                u = 2 * up + uu
+                ps = bank("z", Z_BANKS)
+                for jb in range(NB):
+                    dst = ps[:, P * jb : P * (jb + 1)]
+                    if not on_vector:
+                        nc.tensor.matmul(
+                            dst, lhsT=e_sb[h, g, f0][:, P * jb : P * (jb + 1)], rhs=ident[:],
+                            is_transpose=True, start=True, stop=False,
+                        )
+                    nc.tensor.matmul(
+                        dst, lhsT=p4[h, g, jb, u], rhs=ident[:],
+                        is_transpose=True, start=on_vector, stop=True,
+                    )
+                if on_vector:
+                    nc.vector.tensor_tensor(out=z_sb[n][:, uu, :], in0=ps[:], in1=e_sb[h, g, f0][:], op=ALU.add)
+                else:
+                    nc.scalar.activation(out=t_sb[n][:, uu, :], in_=ps[:], func=ACT.Tanh)
+
+        def tanh_from_sbuf(n):
+            if n in z_sb:
+                t_sb[n] = work.tile([P, 2, HALF], F32, name="t_sb", bufs=4)
+                nc.scalar.activation(out=t_sb[n][:], in_=z_sb[n][:], func=ACT.Tanh)
+
+        def apply_gain(n):
+            h, g, f0, up = pairs[n]
+            if g not in gain_ps:
+                spread_gain(g)
+            y_sb[n] = work.tile([P, 2, HALF], F32, name="y_sb", bufs=YB)
+            nc.vector.tensor_tensor(
+                out=y_sb[n][:], in0=t_sb[n][:], in1=gain_ps[g][:].unsqueeze(1).to_broadcast([P, 2, HALF]), op=ALU.mult
+            )
+            nc.sync.dma_start(out=y_rows[h, f0, :, 2 * up : 2 * up + 2, HALF * g : HALF * (g + 1)], in_=y_sb[n][:])
+
+        def round_y(n):
+            y_bf[n] = work.tile([P, 2 * HALF], BF16, name="y_bf", bufs=5, align_bytes=64)
+            dst = y_bf[n][:].rearrange("q (hh w e) -> q hh w e", hh=2, e=2)
+            src = y_sb[n][:].rearrange("q uu (p hh e) -> q hh (uu p) e", hh=2, e=2)
+            if CAST_ON_GPSIMD and n < n_pairs - TAIL_V:
+                nc.gpsimd.tensor_scalar(out=dst, in0=src, scalar1=1.0, scalar2=-0.0, op0=ALU.mult, op1=ALU.add)
+            else:
+                nc.vector.tensor_copy(out=dst, in_=src)
+
+        def turn_y(n):
+            h, g, f0, up = pairs[n]
+            if (h, g) not in y_grouped:
+                y_grouped[h, g] = work.tile([P, 2048 * 2], F32, name="y_grouped", align_bytes=64)
+            words = y_bf[n][:].bitcast(F32)
+            ps = bank("w", W_BANKS)
+            for blk in range(4):
+                nc.tensor.transpose(ps[:, P * blk : P * (blk + 1)], words[:, P * blk : P * (blk + 1)], ident[:])
+            dst = y_grouped[h, g][:].rearrange("p (q f0 up uu hh) -> p q f0 up uu hh", f0=4, up=2, uu=2, hh=2)
+            nc.scalar.copy(out=dst[:, :, f0, up], in_=ps[:].rearrange("p (hh uu q) -> p q uu hh", hh=2, uu=2))
+
+        y_codes, y_plane = {}, {}
+
+        def quantize_y(h, g, part, parts):
+            width = 2048 // parts
+            if part == 0:
+                y_plane[h, g] = work.tile([P, 2048], U8, name="y_plane", align_bytes=64)
+            codes = work.tile([P, width], U32, name="y_codes", align_bytes=64, bufs=2)
+            nc.vector.quantize_mx(
+                out=codes[:].bitcast(FP8X4),
+                scales=y_plane[h, g][:, width * part : width * (part + 1)],
+                in_=y_grouped[h, g][:, 2 * width * part : 2 * width * (part + 1)].bitcast(BF16),
+            )
+            m0 = 2048 * h + width * part
+            nc.sync.dma_start(out=words_out[g, :, m0 : m0 + width], in_=codes[:].bitcast(I32))
+            if part == parts - 1:
+                for quad in range(4):
+                    nc.sync.dma_start(
+                        out=out_2[g, 4 * quad : 4 * quad + 4, 2048 * h : 2048 * (h + 1)].bitcast(I32),
+                        in_=y_plane[h, g][32 * quad : 32 * quad + 4, :].bitcast(I32),
+                    )
+
+        grouped0 = quantize_wp(0, 0, WP_S)
+        turn_rows(("e", 0, 0), enc_raw[0, 0], CE)
+        finish_wp(0, 0, grouped0)
+        grouped1 = quantize_wp(0, 1)
+        turn_rows(("p", 0, 0), pred_raw[0], CP)
+        quantize_rows(("e", 0, 0), CE)
+        finish_wp(0, 1, grouped1)
+        quantize_rows(("p", 0, 0), CP)
+        turn_bias_gain()
+        first_p = make_p(0, 0, range(NB))
+        make_e(0, 0, 0)
+        for u in range(U):
+            spread_p_by_state(0, 0, u, first_p)
+        turn_rows(("e", 0, 1), enc_raw[0, 1], CE)
+        if SH:
+            sum_z(0)
+        else:
+            quantize_rows(("e", 0, 1), CE)
+            sum_z(0)
+            turn_rows(("e", 0, 3), enc_raw[0, 3], CE)
+            make_e(0, 0, 1)
+
+        n_steps = n_pairs // 2
+        tiles = [(h, g, f0) for (h, g) in groups for f0 in ((0, 1, 2, 3) if SH else (1, 0, 3, 2))]
+        for k in range(n_steps + WB + SH):
+            a, b = 2 * k, 2 * (k - SH) + 1
+            first, second = a - 2, b - 2
+            if 0 <= second and first < n_pairs and pairs[first][1] != pairs[second][1]:
+                first, second = second, first
+            if 0 <= b - 2 < n_pairs:
+                tanh_from_sbuf(b - 2)
+            if 0 <= first < n_pairs:
+                apply_gain(first)
+            if 0 <= b - 2 * WB < n_pairs:
+                turn_y(b - 2 * WB)
+            if 0 <= b < n_pairs:
+                sum_z(b)
+            if 0 <= first < n_pairs:
+                round_y(first)
+            if k + 2 - SH < 8:
+                quantize_rows(("e", tiles[k + 2 - SH][0], tiles[k + 2 - SH][2]), CE)
+            if k == 1:
+                quantize_rows(("p", 1, 0), CP)
+            if k in (WPK, WPK + 1):
+                pending = quantize_wp(1, k - WPK)
+            done = k - QK - WB - SH
+            if done >= 0 and done % 4 in (0, 1) and done // 4 < len(groups) - 1:
+                quantize_y(*groups[done // 4], done % 4, 2)
+            if 0 < a < n_pairs:
+                sum_z(a)
+            if 0 <= second < n_pairs:
+                apply_gain(second)
+            if 0 <= a - 2 * WA < n_pairs:
+                turn_y(a - 2 * WA)
+            if 0 <= second < n_pairs:
+                round_y(second)
+            if k in (WPK, WPK + 1):
+                finish_wp(1, k - WPK, pending)
+            if k + 3 - SH < 8:
+                nxt = tiles[k + 3 - SH]
+                turn_rows(("e", nxt[0], nxt[2]), enc_raw[nxt[0], nxt[2]], CE, ENC_EVAC_V)
+            if k == 0:
+                turn_rows(("p", 1, 0), pred_raw[1], CP)
+            if k + 2 - SH < len(tiles):
+                make_e(*tiles[k + 2 - SH])
+            if k % 4 in (P_K, P_K + 1) and k // 4 + 1 < len(groups):
+                blocks = [2 * (k % 4 - P_K), 2 * (k % 4 - P_K) + 1]
+                ps = make_p(*groups[k // 4 + 1], blocks)
+                for jb in blocks:
+                    spread_p_by_block(*groups[k // 4 + 1], jb, ps)
+        for part in range(QP):
+            quantize_y(*groups[-1], part, QP)

@@ -22,19 +22,22 @@ CE = KE // 512
 CP = KP // 512
 NB = HALF // P
 
-VECTOR_ADD_F0 = (1, 3)
+VECTOR_ADD_F0 = [(1, 3), (1, 3), (1, 3), (1,)]
 CAST_ON_GPSIMD = True
 Z_BANKS, W_BANKS, M_BANKS = 3, 1, 3
 SHARED = True
 WA, WB = 2, 3
 YB = 4
-TAIL_V = 2
+TAIL_V = 1
 WP_S = 128
-QP = 2
+QP = 4
 P_K = 1
 WPK = 3
 QK = 3
 SH = 0
+MID = 0
+WV = 100
+QSPLIT = [(0, 1), (2, 3), (), ()]
 P4B = 8
 ENC_EVAC_V = 0
 
@@ -191,13 +194,15 @@ def tile_transducer_joint_hidden_planes_g5_kernel(
                 out=act_codes[key][:].bitcast(FP8X4), scales=act_plane[key][:], in_=act_grouped[key][:].bitcast(BF16)
             )
 
-        e_sb, p4 = {}, {}
+        e_sb, e_ps, p4 = {}, {}, {}
 
-        def make_e(h, g, f0):
+        def make_e(h, g, f0, part):
             codes, plane = act_codes["e", h, f0], act_plane["e", h, f0]
-            ps = misc_bank()
-            if f0 in VECTOR_ADD_F0:
-                for c in range(CE):
+            if part == 0:
+                e_ps[h, g, f0] = misc_bank()
+            ps = e_ps[h, g, f0]
+            if f0 in VECTOR_ADD_F0[2 * g + h]:
+                for c in (2 * part, 2 * part + 1):
                     nc.tensor.matmul_mx(
                         out=ps[:],
                         lhsT=codes[:, P * c : P * (c + 1)].bitcast(FP8X4),
@@ -208,7 +213,7 @@ def tile_transducer_joint_hidden_planes_g5_kernel(
                         stop=(c == CE - 1),
                     )
             else:
-                for jb in range(NB):
+                for jb in (2 * part, 2 * part + 1):
                     for c in range(CE):
                         j0 = J * c + HALF * g + P * jb
                         nc.tensor.matmul_mx(
@@ -220,8 +225,9 @@ def tile_transducer_joint_hidden_planes_g5_kernel(
                             start=(c == 0),
                             stop=(c == CE - 1),
                         )
-            e_sb[h, g, f0] = work.tile([P, HALF], F32, name="e_sb", bufs=4)
-            nc.scalar.copy(out=e_sb[h, g, f0][:], in_=ps[:])
+            if part == 1:
+                e_sb[h, g, f0] = work.tile([P, HALF], F32, name="e_sb", bufs=4)
+                nc.scalar.copy(out=e_sb[h, g, f0][:], in_=ps[:])
 
         def make_p(h, g, blocks):
             codes, plane = act_codes["p", h, 0], act_plane["p", h, 0]
@@ -259,14 +265,16 @@ def tile_transducer_joint_hidden_planes_g5_kernel(
 
         z_ps, z_sb, t_sb, y_sb, y_bf, y_grouped = {}, {}, {}, {}, {}, {}
 
-        def sum_z(n):
+        def sum_z(n, states=(0, 1)):
             h, g, f0, up = pairs[n]
-            on_vector = f0 in VECTOR_ADD_F0
-            if on_vector:
+            on_vector = f0 in VECTOR_ADD_F0[2 * g + h]
+            if 0 not in states:
+                pass
+            elif on_vector:
                 z_sb[n] = work.tile([P, 2, HALF], F32, name="z_sb")
             else:
                 t_sb[n] = work.tile([P, 2, HALF], F32, name="t_sb", bufs=4)
-            for uu in range(2):
+            for uu in states:
                 u = 2 * up + uu
                 ps = bank("z", Z_BANKS)
                 for jb in range(NB):
@@ -309,7 +317,7 @@ def tile_transducer_joint_hidden_planes_g5_kernel(
             else:
                 nc.vector.tensor_copy(out=dst, in_=src)
 
-        def turn_y(n):
+        def turn_y(n, on_vector=False):
             h, g, f0, up = pairs[n]
             if (h, g) not in y_grouped:
                 y_grouped[h, g] = work.tile([P, 2048 * 2], F32, name="y_grouped", align_bytes=64)
@@ -318,7 +326,7 @@ def tile_transducer_joint_hidden_planes_g5_kernel(
             for blk in range(4):
                 nc.tensor.transpose(ps[:, P * blk : P * (blk + 1)], words[:, P * blk : P * (blk + 1)], ident[:])
             dst = y_grouped[h, g][:].rearrange("p (q f0 up uu hh) -> p q f0 up uu hh", f0=4, up=2, uu=2, hh=2)
-            nc.scalar.copy(out=dst[:, :, f0, up], in_=ps[:].rearrange("p (hh uu q) -> p q uu hh", hh=2, uu=2))
+            copy_out(on_vector, dst[:, :, f0, up], ps[:].rearrange("p (hh uu q) -> p q uu hh", hh=2, uu=2))
 
         y_codes, y_plane = {}, {}
 
@@ -326,7 +334,7 @@ def tile_transducer_joint_hidden_planes_g5_kernel(
             width = 2048 // parts
             if part == 0:
                 y_plane[h, g] = work.tile([P, 2048], U8, name="y_plane", align_bytes=64)
-            codes = work.tile([P, width], U32, name="y_codes", align_bytes=64, bufs=2)
+            codes = work.tile([P, width], U32, name="y_codes", align_bytes=64, bufs=4)
             nc.vector.quantize_mx(
                 out=codes[:].bitcast(FP8X4),
                 scales=y_plane[h, g][:, width * part : width * (part + 1)],
@@ -351,65 +359,70 @@ def tile_transducer_joint_hidden_planes_g5_kernel(
         quantize_rows(("p", 0, 0), CP)
         turn_bias_gain()
         first_p = make_p(0, 0, range(NB))
-        make_e(0, 0, 0)
+        make_e(0, 0, 0, 0)
+        make_e(0, 0, 0, 1)
         for u in range(U):
             spread_p_by_state(0, 0, u, first_p)
         turn_rows(("e", 0, 1), enc_raw[0, 1], CE)
-        if SH:
-            sum_z(0)
-        else:
-            quantize_rows(("e", 0, 1), CE)
-            sum_z(0)
-            turn_rows(("e", 0, 3), enc_raw[0, 3], CE)
-            make_e(0, 0, 1)
+        quantize_rows(("e", 0, 1), CE)
+        sum_z(0)
+        turn_rows(("e", 0, 3), enc_raw[0, 3], CE)
+        make_e(0, 0, 1, 0)
+        make_e(0, 0, 1, 1)
+        quantize_rows(("e", 0, 3), CE)
+        turn_rows(("e", 0, 2), enc_raw[0, 2], CE)
+        make_e(0, 0, 3, 0)
 
         n_steps = n_pairs // 2
-        tiles = [(h, g, f0) for (h, g) in groups for f0 in ((0, 1, 2, 3) if SH else (1, 0, 3, 2))]
-        for k in range(n_steps + WB + SH):
-            a, b = 2 * k, 2 * (k - SH) + 1
-            first, second = a - 2, b - 2
-            if 0 <= second and first < n_pairs and pairs[first][1] != pairs[second][1]:
-                first, second = second, first
-            if 0 <= b - 2 < n_pairs:
+        tiles = [(h, g, f0) for (h, g) in groups for f0 in (1, 0, 3, 2)]
+        for k in range(n_steps + WB):
+            a, b = 2 * k, 2 * k + 1
+            if 1 <= k <= n_steps:
                 tanh_from_sbuf(b - 2)
-            if 0 <= first < n_pairs:
-                apply_gain(first)
+                apply_gain(a - 2)
             if 0 <= b - 2 * WB < n_pairs:
                 turn_y(b - 2 * WB)
-            if 0 <= b < n_pairs:
+            if k < n_steps:
                 sum_z(b)
-            if 0 <= first < n_pairs:
-                round_y(first)
-            if k + 2 - SH < 8:
-                quantize_rows(("e", tiles[k + 2 - SH][0], tiles[k + 2 - SH][2]), CE)
+            if 1 <= k <= n_steps:
+                round_y(a - 2)
+            if k + 3 < 8:
+                quantize_rows(("e", tiles[k + 3][0], tiles[k + 3][2]), CE)
             if k == 1:
                 quantize_rows(("p", 1, 0), CP)
             if k in (WPK, WPK + 1):
                 pending = quantize_wp(1, k - WPK)
-            done = k - QK - WB - SH
-            if done >= 0 and done % 4 in (0, 1) and done // 4 < len(groups) - 1:
-                quantize_y(*groups[done // 4], done % 4, 2)
-            if 0 < a < n_pairs:
-                sum_z(a)
-            if 0 <= second < n_pairs:
-                apply_gain(second)
+            done = k - QK - WB
+            if done >= 0 and done // 4 < len(groups) - 1:
+                for part in QSPLIT[done % 4]:
+                    quantize_y(*groups[done // 4], part, 4)
+            if 0 < k < n_steps:
+                sum_z(a, (0,))
+            if MID == 0 and k + 2 < len(tiles):
+                make_e(*tiles[k + 2], 1)
+            if 0 < k < n_steps:
+                sum_z(a, (1,))
+            if MID == 1 and k + 2 < len(tiles):
+                make_e(*tiles[k + 2], 1)
+            if 1 <= k <= n_steps:
+                apply_gain(b - 2)
             if 0 <= a - 2 * WA < n_pairs:
-                turn_y(a - 2 * WA)
-            if 0 <= second < n_pairs:
-                round_y(second)
+                turn_y(a - 2 * WA, k % WV == WV - 1)
+            if 1 <= k <= n_steps:
+                round_y(b - 2)
             if k in (WPK, WPK + 1):
                 finish_wp(1, k - WPK, pending)
-            if k + 3 - SH < 8:
-                nxt = tiles[k + 3 - SH]
+            if k + 4 < 8:
+                nxt = tiles[k + 4]
                 turn_rows(("e", nxt[0], nxt[2]), enc_raw[nxt[0], nxt[2]], CE, ENC_EVAC_V)
             if k == 0:
                 turn_rows(("p", 1, 0), pred_raw[1], CP)
-            if k + 2 - SH < len(tiles):
-                make_e(*tiles[k + 2 - SH])
             if k % 4 in (P_K, P_K + 1) and k // 4 + 1 < len(groups):
                 blocks = [2 * (k % 4 - P_K), 2 * (k % 4 - P_K) + 1]
                 ps = make_p(*groups[k // 4 + 1], blocks)
                 for jb in blocks:
                     spread_p_by_block(*groups[k // 4 + 1], jb, ps)
+            if k + 3 < len(tiles):
+                make_e(*tiles[k + 3], 0)
         for part in range(QP):
             quantize_y(*groups[-1], part, QP)

@@ -26,16 +26,25 @@ VECTOR_ADD_F0 = [(1, 3), (1, 3), (1, 3), (1,)]
 CAST_ON_GPSIMD = True
 Z_BANKS, W_BANKS, M_BANKS = 3, 1, 3
 SHARED = True
-WA, WB = 2, 3
+WA, WB = 2, 2
 YB = 4
 TAIL_V = 1
 WP_S = 128
 QP = 4
 P_K = 1
-WPK = 3
-QK = 3
+WPK = 1
+QK = 4
 SH = 0
 MID = 0
+QL = 1
+H2 = 1
+ZS = 2
+WPE = False
+WP_S1 = 128
+CS = (31, 32)
+PG = False
+WSWAP = True
+CV = (2, (0,))
 WV = 100
 QSPLIT = [(0, 1), (2, 3), (), ()]
 P4B = 8
@@ -77,9 +86,10 @@ def tile_transducer_joint_hidden_planes_g5_kernel(
 
         ident = keep.tile([P, P], F32, name="ident")
         bg_rows = keep.tile([P, P], BF16, name="bg_rows")
-        we_plane = keep.tile([P, CE * J], U8, name="we_plane", align_bytes=64)
+        we_plane = [keep.tile([P, CE * HALF], U8, name="we_plane%d" % g, align_bytes=64) for g in range(2)]
         nc.vector.memset(bg_rows[:], 0.0)
-        nc.vector.memset(we_plane[:].bitcast(I32), 0)
+        for g in range(2):
+            nc.vector.memset(we_plane[g][:].bitcast(I32), 0)
         make_identity(nc, ident[:])
         warm = keep.tile([P, 1], F32, name="warm")
         nc.scalar.activation(out=warm[:], in_=bg_rows[:, 0:1], func=ACT.Tanh)
@@ -104,25 +114,35 @@ def tile_transducer_joint_hidden_planes_g5_kernel(
             pred_raw[h] = keep.tile([P, KP], BF16, name="pred_raw%d" % h, align_bytes=64)
             nc.sync.dma_start(out=pred_raw[h][:], in_=pred_rows[h])
 
-        load_wp(0, 0)
+        def load_we_scales(g):
+            cols = slice(HALF * g, HALF * (g + 1))
+            plane3 = we_plane[g][:].rearrange("p (c n) -> p c n", c=CE)
+            for quad in range(4):
+                src = we_scales[:, 4 * quad : 4 * quad + 4, cols].rearrange("c r n -> r c n")
+                nc.sync.dma_start(out=plane3[32 * quad : 32 * quad + 4].bitcast(I32), in_=src.bitcast(I32))
+
         load_enc(0, 0)
+        load_wp(0, 0)
+        load_enc(0, 1)
         load_wp(0, 1)
         load_pred(0)
         load_we(0)
-        plane3 = we_plane[:].rearrange("p (c n) -> p c n", c=CE)
-        for quad in range(4):
-            src = we_scales[:, 4 * quad : 4 * quad + 4, :].rearrange("c r n -> r c n")
-            nc.sync.dma_start(out=plane3[32 * quad : 32 * quad + 4].bitcast(I32), in_=src.bitcast(I32))
         nc.sync.dma_start(out=bg_rows[0:8, :], in_=bias.rearrange("(c p) -> c p", p=P))
         nc.sync.dma_start(out=bg_rows[8:16, :], in_=gain.rearrange("(c p) -> c p", p=P))
-        for f0 in ((1, 2, 3) if SH else (1, 3, 2)):
-            load_enc(0, f0)
+        load_we_scales(0)
+        load_enc(0, 3)
+        load_enc(0, 2)
         load_pred(1)
-        for f0 in ((0, 1, 2, 3) if SH else (1, 0, 3, 2)):
+        if WPE:
+            load_wp(1, 0)
+            load_wp(1, 1)
+        for f0 in (1, 0, 3, 2):
             load_enc(1, f0)
-        load_wp(1, 0)
-        load_wp(1, 1)
+        if not WPE:
+            load_wp(1, 0)
+            load_wp(1, 1)
         load_we(1)
+        load_we_scales(1)
 
         bg_cols = keep.tile([P, 16], F32, name="bg_cols")
 
@@ -208,18 +228,18 @@ def tile_transducer_joint_hidden_planes_g5_kernel(
                         lhsT=codes[:, P * c : P * (c + 1)].bitcast(FP8X4),
                         lhsT_scale=plane[:, P * c : P * (c + 1)],
                         rhs=we_codes[g][:, c, :].bitcast(FP4X4),
-                        rhs_scale=we_plane[:, J * c + HALF * g : J * c + HALF * (g + 1)],
+                        rhs_scale=we_plane[g][:, HALF * c : HALF * (c + 1)],
                         start=(c == 0),
                         stop=(c == CE - 1),
                     )
             else:
                 for jb in (2 * part, 2 * part + 1):
                     for c in range(CE):
-                        j0 = J * c + HALF * g + P * jb
+                        j0 = HALF * c + P * jb
                         nc.tensor.matmul_mx(
                             out=ps[:, P * jb : P * (jb + 1)],
                             lhsT=we_codes[g][:, c, 2 * P * jb : 2 * P * (jb + 1)].bitcast(FP4X4),
-                            lhsT_scale=we_plane[:, j0 : j0 + P],
+                            lhsT_scale=we_plane[g][:, j0 : j0 + P],
                             rhs=codes[:, P * c : P * (c + 1)].bitcast(FP8X4),
                             rhs_scale=plane[:, P * c : P * (c + 1)],
                             start=(c == 0),
@@ -255,6 +275,20 @@ def tile_transducer_joint_hidden_planes_g5_kernel(
             for jb in range(NB):
                 p4[h, g, jb, u] = tile[:, jb].rearrange("p i fh -> p (i fh)")
 
+        def spread_p_on_gpsimd(h, g, blocks, ps):
+            small = work.tile([P, 2 * P], F32, name="p_small")
+            nc.scalar.copy(out=small[:], in_=ps[:, P * blocks[0] : P * (blocks[1] + 1)])
+            return small
+
+        def spread_small(h, g, blocks, small):
+            for x, jb in enumerate(blocks):
+                tile = work.tile([P, U, 32, 4], F32, name="p4", bufs=P4B)
+                src = small[:, P * x : P * (x + 1)].rearrange("p (i u) -> p u i", u=U).unsqueeze(3)
+                col = bg_cols[:, NB * g + jb : NB * g + jb + 1]
+                nc.gpsimd.tensor_scalar(out=tile[:], in0=src.to_broadcast([P, U, 32, 4]), scalar1=1.0, scalar2=col, op0=ALU.mult, op1=ALU.add)
+                for u in range(U):
+                    p4[h, g, jb, u] = tile[:, u].rearrange("p i fh -> p (i fh)")
+
         def spread_p_by_block(h, g, jb, ps):
             tile = work.tile([P, U, 32, 4], F32, name="p4", bufs=P4B)
             src = ps[:, P * jb : P * (jb + 1)].rearrange("p (i u) -> p u i", u=U).unsqueeze(3)
@@ -271,7 +305,7 @@ def tile_transducer_joint_hidden_planes_g5_kernel(
             if 0 not in states:
                 pass
             elif on_vector:
-                z_sb[n] = work.tile([P, 2, HALF], F32, name="z_sb")
+                z_sb[n] = work.tile([P, 2, HALF], F32, name="z_sb", bufs=ZS)
             else:
                 t_sb[n] = work.tile([P, 2, HALF], F32, name="t_sb", bufs=4)
             for uu in states:
@@ -309,11 +343,13 @@ def tile_transducer_joint_hidden_planes_g5_kernel(
             nc.sync.dma_start(out=y_rows[h, f0, :, 2 * up : 2 * up + 2, HALF * g : HALF * (g + 1)], in_=y_sb[n][:])
 
         def round_y(n):
-            y_bf[n] = work.tile([P, 2 * HALF], BF16, name="y_bf", bufs=5, align_bytes=64)
+            y_bf[n] = work.tile([P, 2 * HALF], BF16, name="y_bf", bufs=4, align_bytes=64)
             dst = y_bf[n][:].rearrange("q (hh w e) -> q hh w e", hh=2, e=2)
             src = y_sb[n][:].rearrange("q uu (p hh e) -> q hh (uu p) e", hh=2, e=2)
-            if CAST_ON_GPSIMD and n < n_pairs - TAIL_V:
+            if CAST_ON_GPSIMD and n < n_pairs - TAIL_V and n % CV[0] not in CV[1]:
                 nc.gpsimd.tensor_scalar(out=dst, in0=src, scalar1=1.0, scalar2=-0.0, op0=ALU.mult, op1=ALU.add)
+            elif CS[0] <= n < CS[1]:
+                nc.scalar.copy(out=dst, in_=src)
             else:
                 nc.vector.tensor_copy(out=dst, in_=src)
 
@@ -334,7 +370,7 @@ def tile_transducer_joint_hidden_planes_g5_kernel(
             width = 2048 // parts
             if part == 0:
                 y_plane[h, g] = work.tile([P, 2048], U8, name="y_plane", align_bytes=64)
-            codes = work.tile([P, width], U32, name="y_codes", align_bytes=64, bufs=4)
+            codes = work.tile([P, width], U32, name="y_codes", align_bytes=64, bufs=6)
             nc.vector.quantize_mx(
                 out=codes[:].bitcast(FP8X4),
                 scales=y_plane[h, g][:, width * part : width * (part + 1)],
@@ -349,40 +385,44 @@ def tile_transducer_joint_hidden_planes_g5_kernel(
                         in_=y_plane[h, g][32 * quad : 32 * quad + 4, :].bitcast(I32),
                     )
 
-        grouped0 = quantize_wp(0, 0, WP_S)
         turn_rows(("e", 0, 0), enc_raw[0, 0], CE)
-        finish_wp(0, 0, grouped0)
-        grouped1 = quantize_wp(0, 1)
-        turn_rows(("p", 0, 0), pred_raw[0], CP)
+        grouped0 = quantize_wp(0, 0, WP_S)
         quantize_rows(("e", 0, 0), CE)
+        turn_rows(("e", 0, 1), enc_raw[0, 1], CE)
+        finish_wp(0, 0, grouped0)
+        grouped1 = quantize_wp(0, 1, WP_S1)
+        turn_rows(("p", 0, 0), pred_raw[0], CP)
         finish_wp(0, 1, grouped1)
         quantize_rows(("p", 0, 0), CP)
         turn_bias_gain()
+        quantize_rows(("e", 0, 1), CE)
         first_p = make_p(0, 0, range(NB))
         make_e(0, 0, 0, 0)
         make_e(0, 0, 0, 1)
         for u in range(U):
             spread_p_by_state(0, 0, u, first_p)
-        turn_rows(("e", 0, 1), enc_raw[0, 1], CE)
-        quantize_rows(("e", 0, 1), CE)
-        sum_z(0)
-        turn_rows(("e", 0, 3), enc_raw[0, 3], CE)
         make_e(0, 0, 1, 0)
         make_e(0, 0, 1, 1)
+        spread_gain(0)
+        sum_z(0)
+        turn_rows(("e", 0, 3), enc_raw[0, 3], CE)
         quantize_rows(("e", 0, 3), CE)
+        if H2:
+            sum_z(1)
         turn_rows(("e", 0, 2), enc_raw[0, 2], CE)
         make_e(0, 0, 3, 0)
 
         n_steps = n_pairs // 2
         tiles = [(h, g, f0) for (h, g) in groups for f0 in (1, 0, 3, 2)]
-        for k in range(n_steps + WB):
+        for k in range(n_steps):
             a, b = 2 * k, 2 * k + 1
             if 1 <= k <= n_steps:
                 tanh_from_sbuf(b - 2)
                 apply_gain(a - 2)
-            if 0 <= b - 2 * WB < n_pairs:
-                turn_y(b - 2 * WB)
-            if k < n_steps:
+            w1, w2 = (a - 2 * WA, b - 2 * WB) if WSWAP else (b - 2 * WB, a - 2 * WA)
+            if 0 <= w1 < n_pairs:
+                turn_y(w1)
+            if H2 <= k < n_steps:
                 sum_z(b)
             if 1 <= k <= n_steps:
                 round_y(a - 2)
@@ -393,7 +433,7 @@ def tile_transducer_joint_hidden_planes_g5_kernel(
             if k in (WPK, WPK + 1):
                 pending = quantize_wp(1, k - WPK)
             done = k - QK - WB
-            if done >= 0 and done // 4 < len(groups) - 1:
+            if done >= 0 and k < n_steps - QL:
                 for part in QSPLIT[done % 4]:
                     quantize_y(*groups[done // 4], part, 4)
             if 0 < k < n_steps:
@@ -402,12 +442,13 @@ def tile_transducer_joint_hidden_planes_g5_kernel(
                 make_e(*tiles[k + 2], 1)
             if 0 < k < n_steps:
                 sum_z(a, (1,))
+                tanh_from_sbuf(a)
             if MID == 1 and k + 2 < len(tiles):
                 make_e(*tiles[k + 2], 1)
             if 1 <= k <= n_steps:
                 apply_gain(b - 2)
-            if 0 <= a - 2 * WA < n_pairs:
-                turn_y(a - 2 * WA, k % WV == WV - 1)
+            if 0 <= w2 < n_pairs:
+                turn_y(w2, k % WV == WV - 1)
             if 1 <= k <= n_steps:
                 round_y(b - 2)
             if k in (WPK, WPK + 1):
@@ -420,9 +461,25 @@ def tile_transducer_joint_hidden_planes_g5_kernel(
             if k % 4 in (P_K, P_K + 1) and k // 4 + 1 < len(groups):
                 blocks = [2 * (k % 4 - P_K), 2 * (k % 4 - P_K) + 1]
                 ps = make_p(*groups[k // 4 + 1], blocks)
-                for jb in blocks:
-                    spread_p_by_block(*groups[k // 4 + 1], jb, ps)
+                if PG:
+                    spread_small(*groups[k // 4 + 1], blocks, spread_p_on_gpsimd(*groups[k // 4 + 1], blocks, ps))
+                else:
+                    for jb in blocks:
+                        spread_p_by_block(*groups[k // 4 + 1], jb, ps)
             if k + 3 < len(tiles):
                 make_e(*tiles[k + 3], 0)
+        last = n_pairs - 1
+        apply_gain(last)
+        turn_y(last - 3)
+        round_y(last)
+        apply_gain(last - 1)
+        turn_y(last - 2)
+        round_y(last - 1)
+        turn_y(last)
+        if QL:
+            quantize_y(*groups[-2], 2, 4)
+        turn_y(last - 1)
+        if QL:
+            quantize_y(*groups[-2], 3, 4)
         for part in range(QP):
             quantize_y(*groups[-1], part, QP)

@@ -16,59 +16,46 @@ FP4X4 = mybir.dt.float4_e2m1fn_x4
 ACT = mybir.ActivationFunctionType
 ALU = mybir.AluOpType
 
-P = 128
-HALF = 512
-CE = KE // 512
-CP = KP // 512
-NB = HALF // P
+PARTS = 128
+K_PASS = 512
+BANK = 512
+ENC_PASSES = KE // K_PASS
+PRED_PASSES = KP // K_PASS
+BLOCKS = BANK // PARTS
+UTTS = B // 2
+REPEAT = PARTS // UTTS
+GROUP_ROWS = UTTS * T * U
+PLANE_PARTS = 4
+RING_BANKS = 7
 
-VECTOR_ADD_F0 = [(1, 3), (1, 3), (1, 3), (1,)]
-CAST_ON_GPSIMD = True
-Z_BANKS, W_BANKS, M_BANKS = 3, 1, 3
-SHARED = True
-WA, WB = 2, 2
-YB = 4
-TAIL_V = 1
-WP_S = 128
-QP = 4
-P_K = 1
-WPK = 1
-QK = 4
-SH = 0
-MID = 0
-QL = 1
-H2 = 1
-ZS = 2
-WPE = False
-WP_S1 = 128
-CS = (31, 32)
-PG = False
-WSWAP = True
-CV = (2, (0,))
-WV = 100
-QSPLIT = [(0, 1), (2, 3), (), ()]
-P4B = 8
-ENC_EVAC_V = 0
+GROUPS = [(0, 0), (1, 0), (0, 1), (1, 1)]
+PERIODS_PER_GROUP = 4
+LAST_TILE = GROUPS[-1] + (REPEAT - 1,)
+WP_SCALAR_COLUMNS = 128
+SORTED_TILES = [(0, 3), (0, 2), (1, 1)]
+P_BLOCKS_FIRST = [(), (0, 1), (2, 3), ()]
+P_BLOCKS_LATER = [(0,), (1,), (2, 3), ()]
 
 
 def tile_transducer_joint_hidden_planes_g5_kernel(
     tc, enc, we_words, we_scales, pred, wp, bias, gain, out_0, out_1, out_2
 ):
     nc = tc.nc
-    enc_rows = enc.rearrange("(h i) (fh f0) k -> h f0 (i fh) k", h=2, f0=4)
+    enc_rows = enc.rearrange("(h i) (fh r) k -> h r (i fh) k", h=2, r=REPEAT)
     pred_rows = pred.rearrange("(h i) u k -> h (i u) k", h=2)
-    y_rows = out_0.rearrange("(h i) (fh f0) u j -> h f0 (i fh) u j", h=2, f0=4)
+    y_rows = out_0.rearrange("(h i) (fh r) u j -> h r (i fh) u j", h=2, r=REPEAT)
     words_out = out_1.rearrange("g p m t -> g p (m t)").bitcast(I32)
 
-    groups = [(0, 0), (1, 0), (0, 1), (1, 1)]
     pairs = [
-        (h, g, 2 * a + odd, up)
-        for (h, g) in groups
-        for a in range(2)
+        (h, g, 2 * tile_pair + odd, up)
+        for (h, g) in GROUPS
+        for tile_pair in range(2)
         for up in range(2)
         for odd in range(2)
     ]
-    n_pairs = len(pairs)
+
+    def added_on_vector(h, g, r):
+        return r % 2 == 1 and (h, g, r) != LAST_TILE
 
     with ExitStack() as ctx:
         keep = ctx.enter_context(tc.tile_pool(name="keep", bufs=1))
@@ -76,50 +63,288 @@ def tile_transducer_joint_hidden_planes_g5_kernel(
         psum = ctx.enter_context(tc.psum_pool(name="psum", bufs=1))
         ctx.enter_context(tc.manual_schedule())
 
-        def bank(tag, bufs):
-            if SHARED and tag != "gain":
-                return psum.tile([P, HALF], F32, name="ring", tag="ring", bufs=7)
-            return psum.tile([P, HALF], F32, name=tag, tag=tag, bufs=bufs)
+        def next_bank():
+            return psum.tile([PARTS, BANK], F32, name="ring", bufs=RING_BANKS)
 
-        def misc_bank():
-            return bank("misc", M_BANKS)
-
-        ident = keep.tile([P, P], F32, name="ident")
-        bg_rows = keep.tile([P, P], BF16, name="bg_rows")
-        we_plane = [keep.tile([P, CE * HALF], U8, name="we_plane%d" % g, align_bytes=64) for g in range(2)]
-        nc.vector.memset(bg_rows[:], 0.0)
+        ident = keep.tile([PARTS, PARTS], F32, name="ident")
+        vector_rows = keep.tile([PARTS, PARTS], BF16, name="vector_rows")
+        we_plane = [keep.tile([PARTS, ENC_PASSES * BANK], U8, name="we_plane%d" % g, align_bytes=64) for g in range(2)]
+        nc.vector.memset(vector_rows[:], 0.0)
         for g in range(2):
             nc.vector.memset(we_plane[g][:].bitcast(I32), 0)
         make_identity(nc, ident[:])
-        warm = keep.tile([P, 1], F32, name="warm")
-        nc.scalar.activation(out=warm[:], in_=bg_rows[:, 0:1], func=ACT.Tanh)
 
         wp_raw, we_codes, enc_raw, pred_raw = {}, {}, {}, {}
 
         def load_wp(g, c):
-            wp_raw[g, c] = keep.tile([P, 4, HALF], BF16, name="wp_raw%d%d" % (g, c), align_bytes=64)
-            src = wp[512 * c : 512 * (c + 1), HALF * g : HALF * (g + 1)]
+            wp_raw[g, c] = keep.tile([PARTS, 4, BANK], BF16, name="wp_raw%d%d" % (g, c), align_bytes=64)
+            src = wp[K_PASS * c : K_PASS * (c + 1), BANK * g : BANK * (g + 1)]
             nc.sync.dma_start(out=wp_raw[g, c][:], in_=src.rearrange("(p t) n -> p t n", t=4))
 
         def load_we(g):
-            we_codes[g] = keep.tile([P, CE, 2 * HALF], U8, name="we_codes%d" % g, align_bytes=64)
-            src = we_words[:, :, 2 * HALF * g : 2 * HALF * (g + 1)].rearrange("c p n -> p c n")
+            we_codes[g] = keep.tile([PARTS, ENC_PASSES, 2 * BANK], U8, name="we_codes%d" % g, align_bytes=64)
+            src = we_words[:, :, 2 * BANK * g : 2 * BANK * (g + 1)].rearrange("c p n -> p c n")
             nc.sync.dma_start(out=we_codes[g][:].bitcast(I32), in_=src.bitcast(I32))
 
-        def load_enc(h, f0):
-            enc_raw[h, f0] = keep.tile([P, KE], BF16, name="enc_raw%d%d" % (h, f0), align_bytes=64)
-            nc.sync.dma_start(out=enc_raw[h, f0][:], in_=enc_rows[h, f0])
+        def load_we_scales(g):
+            plane = we_plane[g][:].rearrange("p (c n) -> p c n", c=ENC_PASSES)
+            for quad in range(4):
+                src = we_scales[:, 4 * quad : 4 * quad + 4, BANK * g : BANK * (g + 1)].rearrange("c s n -> s c n")
+                nc.sync.dma_start(out=plane[32 * quad : 32 * quad + 4].bitcast(I32), in_=src.bitcast(I32))
+
+        def load_enc(h, r):
+            enc_raw[h, r] = work.tile([PARTS, KE], BF16, name="enc_raw", align_bytes=64, bufs=6)
+            nc.sync.dma_start(out=enc_raw[h, r][:], in_=enc_rows[h, r])
 
         def load_pred(h):
-            pred_raw[h] = keep.tile([P, KP], BF16, name="pred_raw%d" % h, align_bytes=64)
+            pred_raw[h] = keep.tile([PARTS, KP], BF16, name="pred_raw%d" % h, align_bytes=64)
             nc.sync.dma_start(out=pred_raw[h][:], in_=pred_rows[h])
 
-        def load_we_scales(g):
-            cols = slice(HALF * g, HALF * (g + 1))
-            plane3 = we_plane[g][:].rearrange("p (c n) -> p c n", c=CE)
-            for quad in range(4):
-                src = we_scales[:, 4 * quad : 4 * quad + 4, cols].rearrange("c r n -> r c n")
-                nc.sync.dma_start(out=plane3[32 * quad : 32 * quad + 4].bitcast(I32), in_=src.bitcast(I32))
+        vector_cols = keep.tile([PARTS, 16], F32, name="vector_cols")
+        gain_bank = {}
+
+        def turn_bias_and_gain():
+            rows32 = keep.tile([PARTS, PARTS], F32, name="rows32")
+            nc.vector.tensor_copy(out=rows32[:], in_=vector_rows[:])
+            ps = next_bank()
+            nc.tensor.transpose(ps[:, 0:PARTS], rows32[:], ident[:])
+            nc.scalar.copy(out=vector_cols[:], in_=ps[:, 0:16])
+
+        def spread_gain(g):
+            gain_bank[g] = psum.tile([PARTS, BANK], F32, name="gain", bufs=1)
+            for jb in range(BLOCKS):
+                col = 8 + BLOCKS * g + jb
+                nc.tensor.transpose(
+                    gain_bank[g][:, PARTS * jb : PARTS * (jb + 1)],
+                    vector_cols[:, col : col + 1].to_broadcast([PARTS, PARTS]),
+                    ident[:],
+                )
+
+        wp_grouped, wp_codes, wp_plane = {}, {}, {}
+
+        def interleave_wp(g, c, scalar_columns):
+            wp_grouped[g, c] = work.tile([PARTS, BANK * 4], BF16, name="wp_grouped", align_bytes=64)
+            dst = wp_grouped[g, c][:].rearrange("p (n x t) -> p n t x", x=4, t=4)
+            src = wp_raw[g, c][:].rearrange("p t (n x) -> p n t x", x=4)
+            cut = (BANK - scalar_columns) // 4
+            nc.vector.tensor_copy(out=dst[:, :cut], in_=src[:, :cut])
+            if scalar_columns:
+                nc.scalar.copy(out=dst[:, cut:], in_=src[:, cut:])
+
+        def quantize_wp(g, c):
+            wp_codes[g, c] = keep.tile([PARTS, BANK], U32, name="wp_codes%d%d" % (g, c), align_bytes=64)
+            wp_plane[g, c] = keep.tile([PARTS, BANK], U8, name="wp_plane%d%d" % (g, c), align_bytes=64)
+            nc.vector.quantize_mx(
+                out=wp_codes[g, c][:].bitcast(FP8X4), scales=wp_plane[g, c][:], in_=wp_grouped[g, c][:]
+            )
+
+        sorted_words, row_grouped, row_codes, row_plane = {}, {}, {}, {}
+
+        def sort_enc_words(h, r):
+            sorted_words[h, r] = work.tile([PARTS, KE // 2], F32, name="sorted_words", align_bytes=64)
+            nc.vector.tensor_copy(
+                out=sorted_words[h, r][:].rearrange("q (c hh p) -> q c hh p", hh=2, p=PARTS),
+                in_=enc_raw[h, r][:].bitcast(F32).rearrange("q (c p hh) -> q c hh p", hh=2, p=PARTS),
+            )
+
+        def turn_rows(key, passes, words_of):
+            row_grouped[key] = work.tile([PARTS, passes * 2 * PARTS], F32, name="row_grouped", align_bytes=64, bufs=3)
+            for two in range(passes // 2):
+                ps = next_bank()
+                for slot in range(4):
+                    nc.tensor.transpose(
+                        ps[:, PARTS * slot : PARTS * (slot + 1)], words_of(2 * two + slot // 2, slot % 2), ident[:]
+                    )
+                nc.scalar.copy(
+                    out=row_grouped[key][:, BANK * two : BANK * (two + 1)].rearrange("p (c q hh) -> p c q hh", c=2, hh=2),
+                    in_=ps[:].rearrange("p (c hh q) -> p c q hh", c=2, hh=2),
+                )
+
+        def every_second_word(raw):
+            words = raw[:].bitcast(F32)
+            return lambda c, hh: words[:, 256 * c + hh : 256 * (c + 1) : 2]
+
+        def turn_enc(h, r):
+            if (h, r) in SORTED_TILES:
+                words = sorted_words[h, r]
+                turn_rows(("enc", h, r), ENC_PASSES, lambda c, hh: words[:, 256 * c + PARTS * hh : 256 * c + PARTS * (hh + 1)])
+            else:
+                turn_rows(("enc", h, r), ENC_PASSES, every_second_word(enc_raw[h, r]))
+
+        def turn_pred(h):
+            turn_rows(("pred", h, 0), PRED_PASSES, every_second_word(pred_raw[h]))
+
+        def quantize_rows(key, passes):
+            name = "%s%d%d" % key
+            row_codes[key] = keep.tile([PARTS, passes * PARTS], U32, name=name + "_codes", align_bytes=64)
+            row_plane[key] = keep.tile([PARTS, passes * PARTS], U8, name=name + "_plane", align_bytes=64)
+            nc.vector.quantize_mx(
+                out=row_codes[key][:].bitcast(FP8X4), scales=row_plane[key][:], in_=row_grouped[key][:].bitcast(BF16)
+            )
+
+        def quantize_enc(h, r):
+            quantize_rows(("enc", h, r), ENC_PASSES)
+
+        def quantize_pred(h):
+            quantize_rows(("pred", h, 0), PRED_PASSES)
+
+        e_bank, e_sb, p_columns = {}, {}, {}
+
+        def make_e(h, g, r, half):
+            codes, plane = row_codes["enc", h, r], row_plane["enc", h, r]
+            if half == 0:
+                e_bank[h, g, r] = next_bank()
+            ps = e_bank[h, g, r]
+            if added_on_vector(h, g, r):
+                for c in (2 * half, 2 * half + 1):
+                    nc.tensor.matmul_mx(
+                        out=ps[:],
+                        lhsT=codes[:, PARTS * c : PARTS * (c + 1)].bitcast(FP8X4),
+                        lhsT_scale=plane[:, PARTS * c : PARTS * (c + 1)],
+                        rhs=we_codes[g][:, c, :].bitcast(FP4X4),
+                        rhs_scale=we_plane[g][:, BANK * c : BANK * (c + 1)],
+                        start=(c == 0),
+                        stop=(c == ENC_PASSES - 1),
+                    )
+            else:
+                for jb in (2 * half, 2 * half + 1):
+                    for c in range(ENC_PASSES):
+                        first = BANK * c + PARTS * jb
+                        nc.tensor.matmul_mx(
+                            out=ps[:, PARTS * jb : PARTS * (jb + 1)],
+                            lhsT=we_codes[g][:, c, 2 * PARTS * jb : 2 * PARTS * (jb + 1)].bitcast(FP4X4),
+                            lhsT_scale=we_plane[g][:, first : first + PARTS],
+                            rhs=codes[:, PARTS * c : PARTS * (c + 1)].bitcast(FP8X4),
+                            rhs_scale=plane[:, PARTS * c : PARTS * (c + 1)],
+                            start=(c == 0),
+                            stop=(c == ENC_PASSES - 1),
+                        )
+            if half == 1:
+                e_sb[h, g, r] = work.tile([PARTS, BANK], F32, name="e_sb", bufs=4)
+                nc.scalar.copy(out=e_sb[h, g, r][:], in_=ps[:])
+
+        def make_p(h, g, blocks):
+            codes, plane = row_codes["pred", h, 0], row_plane["pred", h, 0]
+            ps = next_bank()
+            for jb in blocks:
+                for c in range(PRED_PASSES):
+                    nc.tensor.matmul_mx(
+                        out=ps[:, PARTS * jb : PARTS * (jb + 1)],
+                        lhsT=wp_codes[g, c][:, PARTS * jb : PARTS * (jb + 1)].bitcast(FP8X4),
+                        lhsT_scale=wp_plane[g, c][:, PARTS * jb : PARTS * (jb + 1)],
+                        rhs=codes[:, PARTS * c : PARTS * (c + 1)].bitcast(FP8X4),
+                        rhs_scale=plane[:, PARTS * c : PARTS * (c + 1)],
+                        start=(c == 0),
+                        stop=(c == PRED_PASSES - 1),
+                    )
+            return ps
+
+        def repeat_p_for_state(h, g, u, ps):
+            tile = work.tile([PARTS, BLOCKS, UTTS, REPEAT], F32, name="p_repeated", bufs=8)
+            src = ps[:].rearrange("p (jb i u) -> p jb i u", jb=BLOCKS, u=U)[:, :, :, u : u + 1]
+            cols = vector_cols[:, BLOCKS * g : BLOCKS * (g + 1)].unsqueeze(2).unsqueeze(3)
+            shape = [PARTS, BLOCKS, UTTS, REPEAT]
+            nc.vector.tensor_tensor(out=tile[:], in0=src.to_broadcast(shape), in1=cols.to_broadcast(shape), op=ALU.add)
+            for jb in range(BLOCKS):
+                p_columns[h, g, jb, u] = tile[:, jb].rearrange("p i fh -> p (i fh)")
+
+        def repeat_p_for_block(h, g, jb, ps):
+            tile = work.tile([PARTS, U, UTTS, REPEAT], F32, name="p_repeated", bufs=8)
+            src = ps[:, PARTS * jb : PARTS * (jb + 1)].rearrange("p (i u) -> p u i", u=U).unsqueeze(3)
+            col = vector_cols[:, BLOCKS * g + jb : BLOCKS * g + jb + 1]
+            nc.scalar.activation(
+                out=tile[:], in_=src.to_broadcast([PARTS, U, UTTS, REPEAT]), func=ACT.Identity, bias=col
+            )
+            for u in range(U):
+                p_columns[h, g, jb, u] = tile[:, u].rearrange("p i fh -> p (i fh)")
+
+        z_sb, tanh_sb, y_sb, y_rounded, y_grouped, y_plane = {}, {}, {}, {}, {}, {}
+
+        def new_tanh_tile(n):
+            tanh_sb[n] = work.tile([PARTS, 2, BANK], F32, name="tanh_sb", bufs=4)
+
+        def sum_state(n, uu):
+            h, g, r, up = pairs[n]
+            on_vector = added_on_vector(h, g, r)
+            if uu == 0 and on_vector:
+                z_sb[n] = work.tile([PARTS, 2, BANK], F32, name="z_sb")
+            elif uu == 0:
+                new_tanh_tile(n)
+            ps = next_bank()
+            for jb in range(BLOCKS):
+                dst = ps[:, PARTS * jb : PARTS * (jb + 1)]
+                if not on_vector:
+                    nc.tensor.matmul(
+                        dst, lhsT=e_sb[h, g, r][:, PARTS * jb : PARTS * (jb + 1)], rhs=ident[:],
+                        is_transpose=True, start=True, stop=False,
+                    )
+                nc.tensor.matmul(
+                    dst, lhsT=p_columns[h, g, jb, 2 * up + uu], rhs=ident[:],
+                    is_transpose=True, start=on_vector, stop=True,
+                )
+            if on_vector:
+                nc.vector.tensor_tensor(out=z_sb[n][:, uu, :], in0=ps[:], in1=e_sb[h, g, r][:], op=ALU.add)
+            else:
+                nc.scalar.activation(out=tanh_sb[n][:, uu, :], in_=ps[:], func=ACT.Tanh)
+
+        def sum_pair(n):
+            sum_state(n, 0)
+            sum_state(n, 1)
+
+        def tanh_after_vector_add(n):
+            new_tanh_tile(n)
+            nc.scalar.activation(out=tanh_sb[n][:], in_=z_sb[n][:], func=ACT.Tanh)
+
+        def apply_gain(n):
+            h, g, r, up = pairs[n]
+            y_sb[n] = work.tile([PARTS, 2, BANK], F32, name="y_sb", bufs=4)
+            nc.vector.tensor_tensor(
+                out=y_sb[n][:], in0=tanh_sb[n][:], in1=gain_bank[g][:].unsqueeze(1).to_broadcast([PARTS, 2, BANK]),
+                op=ALU.mult,
+            )
+            nc.sync.dma_start(out=y_rows[h, r, :, 2 * up : 2 * up + 2, BANK * g : BANK * (g + 1)], in_=y_sb[n][:])
+
+        def round_y(n):
+            y_rounded[n] = work.tile([PARTS, 2 * BANK], BF16, name="y_rounded", bufs=4, align_bytes=64)
+            dst = y_rounded[n][:].rearrange("q (hh w e) -> q hh w e", hh=2, e=2)
+            src = y_sb[n][:].rearrange("q uu (p hh e) -> q hh (uu p) e", hh=2, e=2)
+            if n == len(pairs) - 1:
+                nc.scalar.copy(out=dst, in_=src)
+            elif n % 2 == 1:
+                nc.gpsimd.tensor_scalar(out=dst, in0=src, scalar1=1.0, scalar2=-0.0, op0=ALU.mult, op1=ALU.add)
+            else:
+                nc.vector.tensor_copy(out=dst, in_=src)
+
+        def turn_y(n):
+            h, g, r, up = pairs[n]
+            if (h, g) not in y_grouped:
+                y_grouped[h, g] = work.tile([PARTS, GROUP_ROWS * 2], F32, name="y_grouped", align_bytes=64)
+            words = y_rounded[n][:].bitcast(F32)
+            ps = next_bank()
+            for slot in range(4):
+                cols = slice(PARTS * slot, PARTS * (slot + 1))
+                nc.tensor.transpose(ps[:, cols], words[:, cols], ident[:])
+            dst = y_grouped[h, g][:].rearrange("p (q r up uu hh) -> p q r up uu hh", r=REPEAT, up=2, uu=2, hh=2)
+            nc.scalar.copy(out=dst[:, :, r, up], in_=ps[:].rearrange("p (hh uu q) -> p q uu hh", hh=2, uu=2))
+
+        def quantize_y(h, g, part):
+            width = GROUP_ROWS // PLANE_PARTS
+            if part == 0:
+                y_plane[h, g] = work.tile([PARTS, GROUP_ROWS], U8, name="y_plane", align_bytes=64)
+            codes = work.tile([PARTS, width], U32, name="y_codes", align_bytes=64, bufs=6)
+            nc.vector.quantize_mx(
+                out=codes[:].bitcast(FP8X4),
+                scales=y_plane[h, g][:, width * part : width * (part + 1)],
+                in_=y_grouped[h, g][:, 2 * width * part : 2 * width * (part + 1)].bitcast(BF16),
+            )
+            first = GROUP_ROWS * h + width * part
+            nc.sync.dma_start(out=words_out[g, :, first : first + width], in_=codes[:].bitcast(I32))
+            if part == PLANE_PARTS - 1:
+                for quad in range(4):
+                    nc.sync.dma_start(
+                        out=out_2[g, 4 * quad : 4 * quad + 4, GROUP_ROWS * h : GROUP_ROWS * (h + 1)].bitcast(I32),
+                        in_=y_plane[h, g][32 * quad : 32 * quad + 4, :].bitcast(I32),
+                    )
 
         load_enc(0, 0)
         load_wp(0, 0)
@@ -127,348 +352,102 @@ def tile_transducer_joint_hidden_planes_g5_kernel(
         load_wp(0, 1)
         load_pred(0)
         load_we(0)
-        nc.sync.dma_start(out=bg_rows[0:8, :], in_=bias.rearrange("(c p) -> c p", p=P))
-        nc.sync.dma_start(out=bg_rows[8:16, :], in_=gain.rearrange("(c p) -> c p", p=P))
+        nc.sync.dma_start(out=vector_rows[0:8, :], in_=bias.rearrange("(c p) -> c p", p=PARTS))
+        nc.sync.dma_start(out=vector_rows[8:16, :], in_=gain.rearrange("(c p) -> c p", p=PARTS))
         load_we_scales(0)
         load_enc(0, 3)
         load_enc(0, 2)
         load_pred(1)
-        if WPE:
-            load_wp(1, 0)
-            load_wp(1, 1)
-        for f0 in (1, 0, 3, 2):
-            load_enc(1, f0)
-        if not WPE:
-            load_wp(1, 0)
-            load_wp(1, 1)
+        load_enc(1, 1)
+        load_enc(1, 0)
+
+        turn_enc(0, 0)
+        interleave_wp(0, 0, WP_SCALAR_COLUMNS)
+        quantize_enc(0, 0)
+        turn_enc(0, 1)
+        load_enc(1, 3)
+        load_enc(1, 2)
+        load_wp(1, 0)
+        load_wp(1, 1)
         load_we(1)
         load_we_scales(1)
-
-        bg_cols = keep.tile([P, 16], F32, name="bg_cols")
-
-        def turn_bias_gain():
-            bg32 = keep.tile([P, P], F32, name="bg32")
-            nc.vector.tensor_copy(out=bg32[:], in_=bg_rows[:])
-            bg_ps = misc_bank()
-            nc.tensor.transpose(bg_ps[:, 0:P], bg32[:], ident[:])
-            nc.scalar.copy(out=bg_cols[:], in_=bg_ps[:, 0:16])
-
-        gain_ps = {}
-
-        def spread_gain(g):
-            gain_ps[g] = bank("gain", 1)
-            for jb in range(NB):
-                col = 8 + NB * g + jb
-                nc.tensor.transpose(
-                    gain_ps[g][:, P * jb : P * (jb + 1)], bg_cols[:, col : col + 1].to_broadcast([P, P]), ident[:]
-                )
-
-        def copy_out(on_vector, out, in_):
-            if on_vector:
-                nc.vector.tensor_copy(out=out, in_=in_)
-            else:
-                nc.scalar.copy(out=out, in_=in_)
-
-        wp_codes, wp_plane = {}, {}
-
-        def quantize_wp(g, c, scalar_cols=0):
-            grouped = work.tile([P, HALF * 4], BF16, name="wp_grouped", align_bytes=64)
-            dst = grouped[:].rearrange("p (n i t) -> p n t i", i=4, t=4)
-            src = wp_raw[g, c][:].rearrange("p t (n i) -> p n t i", i=4)
-            cut = (HALF - scalar_cols) // 4
-            nc.vector.tensor_copy(out=dst[:, :cut], in_=src[:, :cut])
-            if scalar_cols:
-                nc.scalar.copy(out=dst[:, cut:], in_=src[:, cut:])
-            wp_codes[g, c] = keep.tile([P, HALF], U32, name="wp_codes%d%d" % (g, c), align_bytes=64)
-            wp_plane[g, c] = keep.tile([P, HALF], U8, name="wp_plane%d%d" % (g, c), align_bytes=64)
-            return grouped
-
-        def finish_wp(g, c, grouped):
-            nc.vector.quantize_mx(out=wp_codes[g, c][:].bitcast(FP8X4), scales=wp_plane[g, c][:], in_=grouped[:])
-
-        act_grouped, act_codes, act_plane = {}, {}, {}
-
-        def turn_rows(key, raw, passes, on_vector=0):
-            words = raw[:].bitcast(F32)
-            act_grouped[key] = work.tile([P, passes * 2 * P], F32, name="act_grouped", align_bytes=64, bufs=3)
-            for c2 in range(passes // 2):
-                ps = misc_bank()
-                for cc in range(2):
-                    c = 2 * c2 + cc
-                    for hh in range(2):
-                        blk = 2 * cc + hh
-                        nc.tensor.transpose(
-                            ps[:, P * blk : P * (blk + 1)], words[:, 256 * c + hh : 256 * (c + 1) : 2], ident[:]
-                        )
-                copy_out(
-                    c2 < on_vector,
-                    act_grouped[key][:, HALF * c2 : HALF * (c2 + 1)].rearrange("p (c q hh) -> p c q hh", c=2, hh=2),
-                    ps[:].rearrange("p (c hh q) -> p c q hh", c=2, hh=2),
-                )
-
-        def quantize_rows(key, passes):
-            name = "act%s%d%d" % key
-            act_codes[key] = keep.tile([P, passes * P], U32, name=name + "c", align_bytes=64)
-            act_plane[key] = keep.tile([P, passes * P], U8, name=name + "s", align_bytes=64)
-            nc.vector.quantize_mx(
-                out=act_codes[key][:].bitcast(FP8X4), scales=act_plane[key][:], in_=act_grouped[key][:].bitcast(BF16)
-            )
-
-        e_sb, e_ps, p4 = {}, {}, {}
-
-        def make_e(h, g, f0, part):
-            codes, plane = act_codes["e", h, f0], act_plane["e", h, f0]
-            if part == 0:
-                e_ps[h, g, f0] = misc_bank()
-            ps = e_ps[h, g, f0]
-            if f0 in VECTOR_ADD_F0[2 * g + h]:
-                for c in (2 * part, 2 * part + 1):
-                    nc.tensor.matmul_mx(
-                        out=ps[:],
-                        lhsT=codes[:, P * c : P * (c + 1)].bitcast(FP8X4),
-                        lhsT_scale=plane[:, P * c : P * (c + 1)],
-                        rhs=we_codes[g][:, c, :].bitcast(FP4X4),
-                        rhs_scale=we_plane[g][:, HALF * c : HALF * (c + 1)],
-                        start=(c == 0),
-                        stop=(c == CE - 1),
-                    )
-            else:
-                for jb in (2 * part, 2 * part + 1):
-                    for c in range(CE):
-                        j0 = HALF * c + P * jb
-                        nc.tensor.matmul_mx(
-                            out=ps[:, P * jb : P * (jb + 1)],
-                            lhsT=we_codes[g][:, c, 2 * P * jb : 2 * P * (jb + 1)].bitcast(FP4X4),
-                            lhsT_scale=we_plane[g][:, j0 : j0 + P],
-                            rhs=codes[:, P * c : P * (c + 1)].bitcast(FP8X4),
-                            rhs_scale=plane[:, P * c : P * (c + 1)],
-                            start=(c == 0),
-                            stop=(c == CE - 1),
-                        )
-            if part == 1:
-                e_sb[h, g, f0] = work.tile([P, HALF], F32, name="e_sb", bufs=4)
-                nc.scalar.copy(out=e_sb[h, g, f0][:], in_=ps[:])
-
-        def make_p(h, g, blocks):
-            codes, plane = act_codes["p", h, 0], act_plane["p", h, 0]
-            ps = misc_bank()
-            for jb in blocks:
-                for c in range(CP):
-                    nc.tensor.matmul_mx(
-                        out=ps[:, P * jb : P * (jb + 1)],
-                        lhsT=wp_codes[g, c][:, P * jb : P * (jb + 1)].bitcast(FP8X4),
-                        lhsT_scale=wp_plane[g, c][:, P * jb : P * (jb + 1)],
-                        rhs=codes[:, P * c : P * (c + 1)].bitcast(FP8X4),
-                        rhs_scale=plane[:, P * c : P * (c + 1)],
-                        start=(c == 0),
-                        stop=(c == CP - 1),
-                    )
-            return ps
-
-        def spread_p_by_state(h, g, u, ps):
-            tile = work.tile([P, NB, 32, 4], F32, name="p4", bufs=P4B)
-            src = ps[:].rearrange("p (jb i u) -> p jb i u", jb=NB, u=U)[:, :, :, u : u + 1]
-            cols = bg_cols[:, NB * g : NB * (g + 1)].unsqueeze(2).unsqueeze(3)
-            nc.vector.tensor_tensor(
-                out=tile[:], in0=src.to_broadcast([P, NB, 32, 4]), in1=cols.to_broadcast([P, NB, 32, 4]), op=ALU.add
-            )
-            for jb in range(NB):
-                p4[h, g, jb, u] = tile[:, jb].rearrange("p i fh -> p (i fh)")
-
-        def spread_p_on_gpsimd(h, g, blocks, ps):
-            small = work.tile([P, 2 * P], F32, name="p_small")
-            nc.scalar.copy(out=small[:], in_=ps[:, P * blocks[0] : P * (blocks[1] + 1)])
-            return small
-
-        def spread_small(h, g, blocks, small):
-            for x, jb in enumerate(blocks):
-                tile = work.tile([P, U, 32, 4], F32, name="p4", bufs=P4B)
-                src = small[:, P * x : P * (x + 1)].rearrange("p (i u) -> p u i", u=U).unsqueeze(3)
-                col = bg_cols[:, NB * g + jb : NB * g + jb + 1]
-                nc.gpsimd.tensor_scalar(out=tile[:], in0=src.to_broadcast([P, U, 32, 4]), scalar1=1.0, scalar2=col, op0=ALU.mult, op1=ALU.add)
-                for u in range(U):
-                    p4[h, g, jb, u] = tile[:, u].rearrange("p i fh -> p (i fh)")
-
-        def spread_p_by_block(h, g, jb, ps):
-            tile = work.tile([P, U, 32, 4], F32, name="p4", bufs=P4B)
-            src = ps[:, P * jb : P * (jb + 1)].rearrange("p (i u) -> p u i", u=U).unsqueeze(3)
-            col = bg_cols[:, NB * g + jb : NB * g + jb + 1]
-            nc.scalar.activation(out=tile[:], in_=src.to_broadcast([P, U, 32, 4]), func=ACT.Identity, bias=col)
-            for u in range(U):
-                p4[h, g, jb, u] = tile[:, u].rearrange("p i fh -> p (i fh)")
-
-        z_ps, z_sb, t_sb, y_sb, y_bf, y_grouped = {}, {}, {}, {}, {}, {}
-
-        def sum_z(n, states=(0, 1)):
-            h, g, f0, up = pairs[n]
-            on_vector = f0 in VECTOR_ADD_F0[2 * g + h]
-            if 0 not in states:
-                pass
-            elif on_vector:
-                z_sb[n] = work.tile([P, 2, HALF], F32, name="z_sb", bufs=ZS)
-            else:
-                t_sb[n] = work.tile([P, 2, HALF], F32, name="t_sb", bufs=4)
-            for uu in states:
-                u = 2 * up + uu
-                ps = bank("z", Z_BANKS)
-                for jb in range(NB):
-                    dst = ps[:, P * jb : P * (jb + 1)]
-                    if not on_vector:
-                        nc.tensor.matmul(
-                            dst, lhsT=e_sb[h, g, f0][:, P * jb : P * (jb + 1)], rhs=ident[:],
-                            is_transpose=True, start=True, stop=False,
-                        )
-                    nc.tensor.matmul(
-                        dst, lhsT=p4[h, g, jb, u], rhs=ident[:],
-                        is_transpose=True, start=on_vector, stop=True,
-                    )
-                if on_vector:
-                    nc.vector.tensor_tensor(out=z_sb[n][:, uu, :], in0=ps[:], in1=e_sb[h, g, f0][:], op=ALU.add)
-                else:
-                    nc.scalar.activation(out=t_sb[n][:, uu, :], in_=ps[:], func=ACT.Tanh)
-
-        def tanh_from_sbuf(n):
-            if n in z_sb:
-                t_sb[n] = work.tile([P, 2, HALF], F32, name="t_sb", bufs=4)
-                nc.scalar.activation(out=t_sb[n][:], in_=z_sb[n][:], func=ACT.Tanh)
-
-        def apply_gain(n):
-            h, g, f0, up = pairs[n]
-            if g not in gain_ps:
-                spread_gain(g)
-            y_sb[n] = work.tile([P, 2, HALF], F32, name="y_sb", bufs=YB)
-            nc.vector.tensor_tensor(
-                out=y_sb[n][:], in0=t_sb[n][:], in1=gain_ps[g][:].unsqueeze(1).to_broadcast([P, 2, HALF]), op=ALU.mult
-            )
-            nc.sync.dma_start(out=y_rows[h, f0, :, 2 * up : 2 * up + 2, HALF * g : HALF * (g + 1)], in_=y_sb[n][:])
-
-        def round_y(n):
-            y_bf[n] = work.tile([P, 2 * HALF], BF16, name="y_bf", bufs=4, align_bytes=64)
-            dst = y_bf[n][:].rearrange("q (hh w e) -> q hh w e", hh=2, e=2)
-            src = y_sb[n][:].rearrange("q uu (p hh e) -> q hh (uu p) e", hh=2, e=2)
-            if CAST_ON_GPSIMD and n < n_pairs - TAIL_V and n % CV[0] not in CV[1]:
-                nc.gpsimd.tensor_scalar(out=dst, in0=src, scalar1=1.0, scalar2=-0.0, op0=ALU.mult, op1=ALU.add)
-            elif CS[0] <= n < CS[1]:
-                nc.scalar.copy(out=dst, in_=src)
-            else:
-                nc.vector.tensor_copy(out=dst, in_=src)
-
-        def turn_y(n, on_vector=False):
-            h, g, f0, up = pairs[n]
-            if (h, g) not in y_grouped:
-                y_grouped[h, g] = work.tile([P, 2048 * 2], F32, name="y_grouped", align_bytes=64)
-            words = y_bf[n][:].bitcast(F32)
-            ps = bank("w", W_BANKS)
-            for blk in range(4):
-                nc.tensor.transpose(ps[:, P * blk : P * (blk + 1)], words[:, P * blk : P * (blk + 1)], ident[:])
-            dst = y_grouped[h, g][:].rearrange("p (q f0 up uu hh) -> p q f0 up uu hh", f0=4, up=2, uu=2, hh=2)
-            copy_out(on_vector, dst[:, :, f0, up], ps[:].rearrange("p (hh uu q) -> p q uu hh", hh=2, uu=2))
-
-        y_codes, y_plane = {}, {}
-
-        def quantize_y(h, g, part, parts):
-            width = 2048 // parts
-            if part == 0:
-                y_plane[h, g] = work.tile([P, 2048], U8, name="y_plane", align_bytes=64)
-            codes = work.tile([P, width], U32, name="y_codes", align_bytes=64, bufs=6)
-            nc.vector.quantize_mx(
-                out=codes[:].bitcast(FP8X4),
-                scales=y_plane[h, g][:, width * part : width * (part + 1)],
-                in_=y_grouped[h, g][:, 2 * width * part : 2 * width * (part + 1)].bitcast(BF16),
-            )
-            m0 = 2048 * h + width * part
-            nc.sync.dma_start(out=words_out[g, :, m0 : m0 + width], in_=codes[:].bitcast(I32))
-            if part == parts - 1:
-                for quad in range(4):
-                    nc.sync.dma_start(
-                        out=out_2[g, 4 * quad : 4 * quad + 4, 2048 * h : 2048 * (h + 1)].bitcast(I32),
-                        in_=y_plane[h, g][32 * quad : 32 * quad + 4, :].bitcast(I32),
-                    )
-
-        turn_rows(("e", 0, 0), enc_raw[0, 0], CE)
-        grouped0 = quantize_wp(0, 0, WP_S)
-        quantize_rows(("e", 0, 0), CE)
-        turn_rows(("e", 0, 1), enc_raw[0, 1], CE)
-        finish_wp(0, 0, grouped0)
-        grouped1 = quantize_wp(0, 1, WP_S1)
-        turn_rows(("p", 0, 0), pred_raw[0], CP)
-        finish_wp(0, 1, grouped1)
-        quantize_rows(("p", 0, 0), CP)
-        turn_bias_gain()
-        quantize_rows(("e", 0, 1), CE)
-        first_p = make_p(0, 0, range(NB))
+        quantize_wp(0, 0)
+        interleave_wp(0, 1, WP_SCALAR_COLUMNS)
+        turn_pred(0)
+        quantize_wp(0, 1)
+        quantize_pred(0)
+        turn_bias_and_gain()
+        quantize_enc(0, 1)
+        first_p = make_p(0, 0, range(BLOCKS))
         make_e(0, 0, 0, 0)
         make_e(0, 0, 0, 1)
+        sort_enc_words(0, 3)
         for u in range(U):
-            spread_p_by_state(0, 0, u, first_p)
+            repeat_p_for_state(0, 0, u, first_p)
+        sort_enc_words(0, 2)
         make_e(0, 0, 1, 0)
         make_e(0, 0, 1, 1)
+        turn_enc(0, 3)
+        sum_pair(0)
+        quantize_enc(0, 3)
+        sort_enc_words(1, 1)
+        sum_pair(1)
+        turn_enc(0, 2)
         spread_gain(0)
-        sum_z(0)
-        turn_rows(("e", 0, 3), enc_raw[0, 3], CE)
-        quantize_rows(("e", 0, 3), CE)
-        if H2:
-            sum_z(1)
-        turn_rows(("e", 0, 2), enc_raw[0, 2], CE)
         make_e(0, 0, 3, 0)
 
-        n_steps = n_pairs // 2
-        tiles = [(h, g, f0) for (h, g) in groups for f0 in (1, 0, 3, 2)]
-        for k in range(n_steps):
-            a, b = 2 * k, 2 * k + 1
-            if 1 <= k <= n_steps:
-                tanh_from_sbuf(b - 2)
-                apply_gain(a - 2)
-            w1, w2 = (a - 2 * WA, b - 2 * WB) if WSWAP else (b - 2 * WB, a - 2 * WA)
-            if 0 <= w1 < n_pairs:
-                turn_y(w1)
-            if H2 <= k < n_steps:
-                sum_z(b)
-            if 1 <= k <= n_steps:
-                round_y(a - 2)
-            if k + 3 < 8:
-                quantize_rows(("e", tiles[k + 3][0], tiles[k + 3][2]), CE)
+        periods = len(pairs) // 2
+        tiles = [(h, g, r) for (h, g) in GROUPS for r in (1, 0, 3, 2)]
+        enc_tiles = 2 * REPEAT
+        for k in range(periods):
+            even, odd = 2 * k, 2 * k + 1
+            group, step = divmod(k, PERIODS_PER_GROUP)
+            if k >= 1:
+                if odd - 2 in z_sb:
+                    tanh_after_vector_add(odd - 2)
+                if pairs[even - 2][1] not in gain_bank:
+                    spread_gain(pairs[even - 2][1])
+                apply_gain(even - 2)
+            if k >= 2:
+                turn_y(even - 4)
+            if k >= 1:
+                sum_pair(odd)
+                round_y(even - 2)
+            if k + 3 < enc_tiles:
+                quantize_enc(tiles[k + 3][0], tiles[k + 3][2])
             if k == 1:
-                quantize_rows(("p", 1, 0), CP)
-            if k in (WPK, WPK + 1):
-                pending = quantize_wp(1, k - WPK)
-            done = k - QK - WB
-            if done >= 0 and k < n_steps - QL:
-                for part in QSPLIT[done % 4]:
-                    quantize_y(*groups[done // 4], part, 4)
-            if 0 < k < n_steps:
-                sum_z(a, (0,))
-            if MID == 0 and k + 2 < len(tiles):
+                quantize_pred(1)
+            if k in (1, 2):
+                interleave_wp(1, k - 1, 0)
+            if group >= 1 and step >= 2 and k < periods - 1:
+                quantize_y(*GROUPS[group - 1], 2 * (step - 2))
+                quantize_y(*GROUPS[group - 1], 2 * (step - 2) + 1)
+            if k >= 1:
+                sum_state(even, 0)
+            if k + 2 < len(tiles):
                 make_e(*tiles[k + 2], 1)
-            if 0 < k < n_steps:
-                sum_z(a, (1,))
-                tanh_from_sbuf(a)
-            if MID == 1 and k + 2 < len(tiles):
-                make_e(*tiles[k + 2], 1)
-            if 1 <= k <= n_steps:
-                apply_gain(b - 2)
-            if 0 <= w2 < n_pairs:
-                turn_y(w2, k % WV == WV - 1)
-            if 1 <= k <= n_steps:
-                round_y(b - 2)
-            if k in (WPK, WPK + 1):
-                finish_wp(1, k - WPK, pending)
-            if k + 4 < 8:
-                nxt = tiles[k + 4]
-                turn_rows(("e", nxt[0], nxt[2]), enc_raw[nxt[0], nxt[2]], CE, ENC_EVAC_V)
+            if k >= 1:
+                sum_state(even, 1)
+                apply_gain(odd - 2)
+            if k >= 2:
+                turn_y(odd - 4)
+            if k >= 1:
+                round_y(odd - 2)
+            if k in (1, 2):
+                quantize_wp(1, k - 1)
+            if k + 4 < enc_tiles:
+                turn_enc(tiles[k + 4][0], tiles[k + 4][2])
             if k == 0:
-                turn_rows(("p", 1, 0), pred_raw[1], CP)
-            if k % 4 in (P_K, P_K + 1) and k // 4 + 1 < len(groups):
-                blocks = [2 * (k % 4 - P_K), 2 * (k % 4 - P_K) + 1]
-                ps = make_p(*groups[k // 4 + 1], blocks)
-                if PG:
-                    spread_small(*groups[k // 4 + 1], blocks, spread_p_on_gpsimd(*groups[k // 4 + 1], blocks, ps))
-                else:
-                    for jb in blocks:
-                        spread_p_by_block(*groups[k // 4 + 1], jb, ps)
+                turn_pred(1)
+            blocks = (P_BLOCKS_FIRST if group == 0 else P_BLOCKS_LATER)[step]
+            if blocks and group + 1 < len(GROUPS):
+                ps = make_p(*GROUPS[group + 1], blocks)
+                for jb in blocks:
+                    repeat_p_for_block(*GROUPS[group + 1], jb, ps)
             if k + 3 < len(tiles):
                 make_e(*tiles[k + 3], 0)
-        last = n_pairs - 1
+
+        last = len(pairs) - 1
         apply_gain(last)
         turn_y(last - 3)
         round_y(last)
@@ -476,10 +455,8 @@ def tile_transducer_joint_hidden_planes_g5_kernel(
         turn_y(last - 2)
         round_y(last - 1)
         turn_y(last)
-        if QL:
-            quantize_y(*groups[-2], 2, 4)
+        quantize_y(*GROUPS[-2], 2)
         turn_y(last - 1)
-        if QL:
-            quantize_y(*groups[-2], 3, 4)
-        for part in range(QP):
-            quantize_y(*groups[-1], part, QP)
+        quantize_y(*GROUPS[-2], 3)
+        for part in range(PLANE_PARTS):
+            quantize_y(*GROUPS[-1], part)

from contextlib import ExitStack

import concourse.mybir as mybir
from concourse.masks import make_identity

B, T, U, KE, KP, J = 64, 16, 4, 2048, 1024, 1024
FLOPS = 2 * B * T * KE * J + 2 * B * U * KP * J

F32 = mybir.dt.float32
BF16 = mybir.dt.bfloat16
I32 = mybir.dt.int32
U32 = mybir.dt.uint32
U8 = mybir.dt.uint8
FP8X4 = mybir.dt.float8_e4m3fn_x4
FP4X4 = mybir.dt.float4_e2m1fn_x4
ACT = mybir.ActivationFunctionType
ALU = mybir.AluOpType

PARTS = 128
K_PASS = 512
BANK = 512
ENC_PASSES = KE // K_PASS
PRED_PASSES = KP // K_PASS
BLOCKS = BANK // PARTS
UTTS = B // 2
REPEAT = PARTS // UTTS
GROUP_ROWS = UTTS * T * U
PLANE_PARTS = 4
RING_BANKS = 7

GROUPS = [(0, 0), (1, 0), (0, 1), (1, 1)]
PERIODS_PER_GROUP = 4
LAST_TILE = GROUPS[-1] + (REPEAT - 1,)
WP_SCALAR_COLUMNS = 128
SORTED_TILES = [(0, 3), (0, 2), (1, 1)]
P_BLOCKS_FIRST = [(), (0, 1), (2, 3), ()]
P_BLOCKS_LATER = [(0,), (1,), (2, 3), ()]


def tile_transducer_joint_hidden_planes_g5_kernel(
    tc, enc, we_words, we_scales, pred, wp, bias, gain, out_0, out_1, out_2
):
    nc = tc.nc
    enc_rows = enc.rearrange("(h i) (fh r) k -> h r (i fh) k", h=2, r=REPEAT)
    pred_rows = pred.rearrange("(h i) u k -> h (i u) k", h=2)
    y_rows = out_0.rearrange("(h i) (fh r) u j -> h r (i fh) u j", h=2, r=REPEAT)
    words_out = out_1.rearrange("g p m t -> g p (m t)").bitcast(I32)

    pairs = [
        (h, g, 2 * tile_pair + odd, up)
        for (h, g) in GROUPS
        for tile_pair in range(2)
        for up in range(2)
        for odd in range(2)
    ]

    def added_on_vector(h, g, r):
        return r % 2 == 1 and (h, g, r) != LAST_TILE

    with ExitStack() as ctx:
        keep = ctx.enter_context(tc.tile_pool(name="keep", bufs=1))
        work = ctx.enter_context(tc.tile_pool(name="work", bufs=2))
        psum = ctx.enter_context(tc.psum_pool(name="psum", bufs=1))
        ctx.enter_context(tc.manual_schedule())

        def next_bank():
            return psum.tile([PARTS, BANK], F32, name="ring", bufs=RING_BANKS)

        ident = keep.tile([PARTS, PARTS], F32, name="ident")
        vector_rows = keep.tile([PARTS, PARTS], BF16, name="vector_rows")
        we_plane = [keep.tile([PARTS, ENC_PASSES * BANK], U8, name="we_plane%d" % g, align_bytes=64) for g in range(2)]
        nc.vector.memset(vector_rows[:], 0.0)
        for g in range(2):
            nc.vector.memset(we_plane[g][:].bitcast(I32), 0)
        make_identity(nc, ident[:])

        wp_raw, we_codes, enc_raw, pred_raw = {}, {}, {}, {}

        def load_wp(g, c):
            wp_raw[g, c] = keep.tile([PARTS, 4, BANK], BF16, name="wp_raw%d%d" % (g, c), align_bytes=64)
            src = wp[K_PASS * c : K_PASS * (c + 1), BANK * g : BANK * (g + 1)]
            nc.sync.dma_start(out=wp_raw[g, c][:], in_=src.rearrange("(p t) n -> p t n", t=4))

        def load_we(g):
            we_codes[g] = keep.tile([PARTS, ENC_PASSES, 2 * BANK], U8, name="we_codes%d" % g, align_bytes=64)
            src = we_words[:, :, 2 * BANK * g : 2 * BANK * (g + 1)].rearrange("c p n -> p c n")
            nc.sync.dma_start(out=we_codes[g][:].bitcast(I32), in_=src.bitcast(I32))

        def load_we_scales(g):
            plane = we_plane[g][:].rearrange("p (c n) -> p c n", c=ENC_PASSES)
            for quad in range(4):
                src = we_scales[:, 4 * quad : 4 * quad + 4, BANK * g : BANK * (g + 1)].rearrange("c s n -> s c n")
                nc.sync.dma_start(out=plane[32 * quad : 32 * quad + 4].bitcast(I32), in_=src.bitcast(I32))

        def load_enc(h, r):
            enc_raw[h, r] = work.tile([PARTS, KE], BF16, name="enc_raw", align_bytes=64, bufs=6)
            nc.sync.dma_start(out=enc_raw[h, r][:], in_=enc_rows[h, r])

        def load_pred(h):
            pred_raw[h] = keep.tile([PARTS, KP], BF16, name="pred_raw%d" % h, align_bytes=64)
            nc.sync.dma_start(out=pred_raw[h][:], in_=pred_rows[h])

        vector_cols = keep.tile([PARTS, 16], F32, name="vector_cols")
        gain_bank = {}

        def turn_bias_and_gain():
            rows32 = keep.tile([PARTS, PARTS], F32, name="rows32")
            nc.vector.tensor_copy(out=rows32[:], in_=vector_rows[:])
            ps = next_bank()
            nc.tensor.transpose(ps[:, 0:PARTS], rows32[:], ident[:])
            nc.scalar.copy(out=vector_cols[:], in_=ps[:, 0:16])

        def spread_gain(g):
            gain_bank[g] = psum.tile([PARTS, BANK], F32, name="gain", bufs=1)
            for jb in range(BLOCKS):
                col = 8 + BLOCKS * g + jb
                nc.tensor.transpose(
                    gain_bank[g][:, PARTS * jb : PARTS * (jb + 1)],
                    vector_cols[:, col : col + 1].to_broadcast([PARTS, PARTS]),
                    ident[:],
                )

        wp_grouped, wp_codes, wp_plane = {}, {}, {}

        def interleave_wp(g, c, scalar_columns):
            wp_grouped[g, c] = work.tile([PARTS, BANK * 4], BF16, name="wp_grouped", align_bytes=64)
            dst = wp_grouped[g, c][:].rearrange("p (n x t) -> p n t x", x=4, t=4)
            src = wp_raw[g, c][:].rearrange("p t (n x) -> p n t x", x=4)
            cut = (BANK - scalar_columns) // 4
            nc.vector.tensor_copy(out=dst[:, :cut], in_=src[:, :cut])
            if scalar_columns:
                nc.scalar.copy(out=dst[:, cut:], in_=src[:, cut:])

        def quantize_wp(g, c):
            wp_codes[g, c] = keep.tile([PARTS, BANK], U32, name="wp_codes%d%d" % (g, c), align_bytes=64)
            wp_plane[g, c] = keep.tile([PARTS, BANK], U8, name="wp_plane%d%d" % (g, c), align_bytes=64)
            nc.vector.quantize_mx(
                out=wp_codes[g, c][:].bitcast(FP8X4), scales=wp_plane[g, c][:], in_=wp_grouped[g, c][:]
            )

        sorted_words, row_grouped, row_codes, row_plane = {}, {}, {}, {}

        def sort_enc_words(h, r):
            sorted_words[h, r] = work.tile([PARTS, KE // 2], F32, name="sorted_words", align_bytes=64)
            nc.vector.tensor_copy(
                out=sorted_words[h, r][:].rearrange("q (c hh p) -> q c hh p", hh=2, p=PARTS),
                in_=enc_raw[h, r][:].bitcast(F32).rearrange("q (c p hh) -> q c hh p", hh=2, p=PARTS),
            )

        def turn_rows(key, passes, words_of):
            row_grouped[key] = work.tile([PARTS, passes * 2 * PARTS], F32, name="row_grouped", align_bytes=64, bufs=3)
            for two in range(passes // 2):
                ps = next_bank()
                for slot in range(4):
                    nc.tensor.transpose(
                        ps[:, PARTS * slot : PARTS * (slot + 1)], words_of(2 * two + slot // 2, slot % 2), ident[:]
                    )
                nc.scalar.copy(
                    out=row_grouped[key][:, BANK * two : BANK * (two + 1)].rearrange("p (c q hh) -> p c q hh", c=2, hh=2),
                    in_=ps[:].rearrange("p (c hh q) -> p c q hh", c=2, hh=2),
                )

        def every_second_word(raw):
            words = raw[:].bitcast(F32)
            return lambda c, hh: words[:, 256 * c + hh : 256 * (c + 1) : 2]

        def turn_enc(h, r):
            if (h, r) in SORTED_TILES:
                words = sorted_words[h, r]
                turn_rows(("enc", h, r), ENC_PASSES, lambda c, hh: words[:, 256 * c + PARTS * hh : 256 * c + PARTS * (hh + 1)])
            else:
                turn_rows(("enc", h, r), ENC_PASSES, every_second_word(enc_raw[h, r]))

        def turn_pred(h):
            turn_rows(("pred", h, 0), PRED_PASSES, every_second_word(pred_raw[h]))

        def quantize_rows(key, passes):
            name = "%s%d%d" % key
            row_codes[key] = keep.tile([PARTS, passes * PARTS], U32, name=name + "_codes", align_bytes=64)
            row_plane[key] = keep.tile([PARTS, passes * PARTS], U8, name=name + "_plane", align_bytes=64)
            nc.vector.quantize_mx(
                out=row_codes[key][:].bitcast(FP8X4), scales=row_plane[key][:], in_=row_grouped[key][:].bitcast(BF16)
            )

        def quantize_enc(h, r):
            quantize_rows(("enc", h, r), ENC_PASSES)

        def quantize_pred(h):
            quantize_rows(("pred", h, 0), PRED_PASSES)

        e_bank, e_sb, p_columns = {}, {}, {}

        def make_e(h, g, r, half):
            codes, plane = row_codes["enc", h, r], row_plane["enc", h, r]
            if half == 0:
                e_bank[h, g, r] = next_bank()
            ps = e_bank[h, g, r]
            if added_on_vector(h, g, r):
                for c in (2 * half, 2 * half + 1):
                    nc.tensor.matmul_mx(
                        out=ps[:],
                        lhsT=codes[:, PARTS * c : PARTS * (c + 1)].bitcast(FP8X4),
                        lhsT_scale=plane[:, PARTS * c : PARTS * (c + 1)],
                        rhs=we_codes[g][:, c, :].bitcast(FP4X4),
                        rhs_scale=we_plane[g][:, BANK * c : BANK * (c + 1)],
                        start=(c == 0),
                        stop=(c == ENC_PASSES - 1),
                    )
            else:
                for jb in (2 * half, 2 * half + 1):
                    for c in range(ENC_PASSES):
                        first = BANK * c + PARTS * jb
                        nc.tensor.matmul_mx(
                            out=ps[:, PARTS * jb : PARTS * (jb + 1)],
                            lhsT=we_codes[g][:, c, 2 * PARTS * jb : 2 * PARTS * (jb + 1)].bitcast(FP4X4),
                            lhsT_scale=we_plane[g][:, first : first + PARTS],
                            rhs=codes[:, PARTS * c : PARTS * (c + 1)].bitcast(FP8X4),
                            rhs_scale=plane[:, PARTS * c : PARTS * (c + 1)],
                            start=(c == 0),
                            stop=(c == ENC_PASSES - 1),
                        )
            if half == 1:
                e_sb[h, g, r] = work.tile([PARTS, BANK], F32, name="e_sb", bufs=4)
                nc.scalar.copy(out=e_sb[h, g, r][:], in_=ps[:])

        def make_p(h, g, blocks):
            codes, plane = row_codes["pred", h, 0], row_plane["pred", h, 0]
            ps = next_bank()
            for jb in blocks:
                for c in range(PRED_PASSES):
                    nc.tensor.matmul_mx(
                        out=ps[:, PARTS * jb : PARTS * (jb + 1)],
                        lhsT=wp_codes[g, c][:, PARTS * jb : PARTS * (jb + 1)].bitcast(FP8X4),
                        lhsT_scale=wp_plane[g, c][:, PARTS * jb : PARTS * (jb + 1)],
                        rhs=codes[:, PARTS * c : PARTS * (c + 1)].bitcast(FP8X4),
                        rhs_scale=plane[:, PARTS * c : PARTS * (c + 1)],
                        start=(c == 0),
                        stop=(c == PRED_PASSES - 1),
                    )
            return ps

        def repeat_p_for_state(h, g, u, ps):
            tile = work.tile([PARTS, BLOCKS, UTTS, REPEAT], F32, name="p_repeated", bufs=8)
            src = ps[:].rearrange("p (jb i u) -> p jb i u", jb=BLOCKS, u=U)[:, :, :, u : u + 1]
            cols = vector_cols[:, BLOCKS * g : BLOCKS * (g + 1)].unsqueeze(2).unsqueeze(3)
            shape = [PARTS, BLOCKS, UTTS, REPEAT]
            nc.vector.tensor_tensor(out=tile[:], in0=src.to_broadcast(shape), in1=cols.to_broadcast(shape), op=ALU.add)
            for jb in range(BLOCKS):
                p_columns[h, g, jb, u] = tile[:, jb].rearrange("p i fh -> p (i fh)")

        def repeat_p_for_block(h, g, jb, ps):
            tile = work.tile([PARTS, U, UTTS, REPEAT], F32, name="p_repeated", bufs=8)
            src = ps[:, PARTS * jb : PARTS * (jb + 1)].rearrange("p (i u) -> p u i", u=U).unsqueeze(3)
            col = vector_cols[:, BLOCKS * g + jb : BLOCKS * g + jb + 1]
            nc.scalar.activation(
                out=tile[:], in_=src.to_broadcast([PARTS, U, UTTS, REPEAT]), func=ACT.Identity, bias=col
            )
            for u in range(U):
                p_columns[h, g, jb, u] = tile[:, u].rearrange("p i fh -> p (i fh)")

        z_sb, tanh_sb, y_sb, y_rounded, y_grouped, y_plane = {}, {}, {}, {}, {}, {}

        def new_tanh_tile(n):
            tanh_sb[n] = work.tile([PARTS, 2, BANK], F32, name="tanh_sb", bufs=4)

        def sum_state(n, uu):
            h, g, r, up = pairs[n]
            on_vector = added_on_vector(h, g, r)
            if uu == 0 and on_vector:
                z_sb[n] = work.tile([PARTS, 2, BANK], F32, name="z_sb")
            elif uu == 0:
                new_tanh_tile(n)
            ps = next_bank()
            for jb in range(BLOCKS):
                dst = ps[:, PARTS * jb : PARTS * (jb + 1)]
                if not on_vector:
                    nc.tensor.matmul(
                        dst, lhsT=e_sb[h, g, r][:, PARTS * jb : PARTS * (jb + 1)], rhs=ident[:],
                        is_transpose=True, start=True, stop=False,
                    )
                nc.tensor.matmul(
                    dst, lhsT=p_columns[h, g, jb, 2 * up + uu], rhs=ident[:],
                    is_transpose=True, start=on_vector, stop=True,
                )
            if on_vector:
                nc.vector.tensor_tensor(out=z_sb[n][:, uu, :], in0=ps[:], in1=e_sb[h, g, r][:], op=ALU.add)
            else:
                nc.scalar.activation(out=tanh_sb[n][:, uu, :], in_=ps[:], func=ACT.Tanh)

        def sum_pair(n):
            sum_state(n, 0)
            sum_state(n, 1)

        def tanh_after_vector_add(n):
            new_tanh_tile(n)
            nc.scalar.activation(out=tanh_sb[n][:], in_=z_sb[n][:], func=ACT.Tanh)

        def apply_gain(n):
            h, g, r, up = pairs[n]
            y_sb[n] = work.tile([PARTS, 2, BANK], F32, name="y_sb", bufs=4)
            nc.vector.tensor_tensor(
                out=y_sb[n][:], in0=tanh_sb[n][:], in1=gain_bank[g][:].unsqueeze(1).to_broadcast([PARTS, 2, BANK]),
                op=ALU.mult,
            )
            nc.sync.dma_start(out=y_rows[h, r, :, 2 * up : 2 * up + 2, BANK * g : BANK * (g + 1)], in_=y_sb[n][:])

        def round_y(n):
            y_rounded[n] = work.tile([PARTS, 2 * BANK], BF16, name="y_rounded", bufs=4, align_bytes=64)
            dst = y_rounded[n][:].rearrange("q (hh w e) -> q hh w e", hh=2, e=2)
            src = y_sb[n][:].rearrange("q uu (p hh e) -> q hh (uu p) e", hh=2, e=2)
            if n == len(pairs) - 1:
                nc.scalar.copy(out=dst, in_=src)
            elif n % 2 == 1:
                nc.gpsimd.tensor_scalar(out=dst, in0=src, scalar1=1.0, scalar2=-0.0, op0=ALU.mult, op1=ALU.add)
            else:
                nc.vector.tensor_copy(out=dst, in_=src)

        def turn_y(n):
            h, g, r, up = pairs[n]
            if (h, g) not in y_grouped:
                y_grouped[h, g] = work.tile([PARTS, GROUP_ROWS * 2], F32, name="y_grouped", align_bytes=64)
            words = y_rounded[n][:].bitcast(F32)
            ps = next_bank()
            for slot in range(4):
                cols = slice(PARTS * slot, PARTS * (slot + 1))
                nc.tensor.transpose(ps[:, cols], words[:, cols], ident[:])
            dst = y_grouped[h, g][:].rearrange("p (q r up uu hh) -> p q r up uu hh", r=REPEAT, up=2, uu=2, hh=2)
            nc.scalar.copy(out=dst[:, :, r, up], in_=ps[:].rearrange("p (hh uu q) -> p q uu hh", hh=2, uu=2))

        def quantize_y(h, g, part):
            width = GROUP_ROWS // PLANE_PARTS
            if part == 0:
                y_plane[h, g] = work.tile([PARTS, GROUP_ROWS], U8, name="y_plane", align_bytes=64)
            codes = work.tile([PARTS, width], U32, name="y_codes", align_bytes=64, bufs=6)
            nc.vector.quantize_mx(
                out=codes[:].bitcast(FP8X4),
                scales=y_plane[h, g][:, width * part : width * (part + 1)],
                in_=y_grouped[h, g][:, 2 * width * part : 2 * width * (part + 1)].bitcast(BF16),
            )
            first = GROUP_ROWS * h + width * part
            nc.sync.dma_start(out=words_out[g, :, first : first + width], in_=codes[:].bitcast(I32))
            if part == PLANE_PARTS - 1:
                for quad in range(4):
                    nc.sync.dma_start(
                        out=out_2[g, 4 * quad : 4 * quad + 4, GROUP_ROWS * h : GROUP_ROWS * (h + 1)].bitcast(I32),
                        in_=y_plane[h, g][32 * quad : 32 * quad + 4, :].bitcast(I32),
                    )

        load_enc(0, 0)
        load_wp(0, 0)
        load_enc(0, 1)
        load_wp(0, 1)
        load_pred(0)
        load_we(0)
        nc.sync.dma_start(out=vector_rows[0:8, :], in_=bias.rearrange("(c p) -> c p", p=PARTS))
        nc.sync.dma_start(out=vector_rows[8:16, :], in_=gain.rearrange("(c p) -> c p", p=PARTS))
        load_we_scales(0)
        load_enc(0, 3)
        load_enc(0, 2)
        load_pred(1)
        load_enc(1, 1)
        load_enc(1, 0)

        turn_enc(0, 0)
        interleave_wp(0, 0, WP_SCALAR_COLUMNS)
        quantize_enc(0, 0)
        turn_enc(0, 1)
        load_enc(1, 3)
        load_enc(1, 2)
        load_wp(1, 0)
        load_wp(1, 1)
        load_we(1)
        load_we_scales(1)
        quantize_wp(0, 0)
        interleave_wp(0, 1, WP_SCALAR_COLUMNS)
        turn_pred(0)
        quantize_wp(0, 1)
        quantize_pred(0)
        turn_bias_and_gain()
        quantize_enc(0, 1)
        first_p = make_p(0, 0, range(BLOCKS))
        make_e(0, 0, 0, 0)
        make_e(0, 0, 0, 1)
        sort_enc_words(0, 3)
        for u in range(U):
            repeat_p_for_state(0, 0, u, first_p)
        sort_enc_words(0, 2)
        make_e(0, 0, 1, 0)
        make_e(0, 0, 1, 1)
        turn_enc(0, 3)
        sum_pair(0)
        quantize_enc(0, 3)
        sort_enc_words(1, 1)
        sum_pair(1)
        turn_enc(0, 2)
        spread_gain(0)
        make_e(0, 0, 3, 0)

        periods = len(pairs) // 2
        tiles = [(h, g, r) for (h, g) in GROUPS for r in (1, 0, 3, 2)]
        enc_tiles = 2 * REPEAT
        for k in range(periods):
            even, odd = 2 * k, 2 * k + 1
            group, step = divmod(k, PERIODS_PER_GROUP)
            if k >= 1:
                if odd - 2 in z_sb:
                    tanh_after_vector_add(odd - 2)
                if pairs[even - 2][1] not in gain_bank:
                    spread_gain(pairs[even - 2][1])
                apply_gain(even - 2)
            if k >= 2:
                turn_y(even - 4)
            if k >= 1:
                sum_pair(odd)
                round_y(even - 2)
            if k + 3 < enc_tiles:
                quantize_enc(tiles[k + 3][0], tiles[k + 3][2])
            if k == 1:
                quantize_pred(1)
            if k in (1, 2):
                interleave_wp(1, k - 1, 0)
            if group >= 1 and step >= 2 and k < periods - 1:
                quantize_y(*GROUPS[group - 1], 2 * (step - 2))
                quantize_y(*GROUPS[group - 1], 2 * (step - 2) + 1)
            if k >= 1:
                sum_state(even, 0)
            if k + 2 < len(tiles):
                make_e(*tiles[k + 2], 1)
            if k >= 1:
                sum_state(even, 1)
                apply_gain(odd - 2)
            if k >= 2:
                turn_y(odd - 4)
            if k >= 1:
                round_y(odd - 2)
            if k in (1, 2):
                quantize_wp(1, k - 1)
            if k + 4 < enc_tiles:
                turn_enc(tiles[k + 4][0], tiles[k + 4][2])
            if k == 0:
                turn_pred(1)
            blocks = (P_BLOCKS_FIRST if group == 0 else P_BLOCKS_LATER)[step]
            if blocks and group + 1 < len(GROUPS):
                ps = make_p(*GROUPS[group + 1], blocks)
                for jb in blocks:
                    repeat_p_for_block(*GROUPS[group + 1], jb, ps)
            if k + 3 < len(tiles):
                make_e(*tiles[k + 3], 0)

        last = len(pairs) - 1
        apply_gain(last)
        turn_y(last - 3)
        round_y(last)
        apply_gain(last - 1)
        turn_y(last - 2)
        round_y(last - 1)
        turn_y(last)
        quantize_y(*GROUPS[-2], 2)
        turn_y(last - 1)
        quantize_y(*GROUPS[-2], 3)
        for part in range(PLANE_PARTS):
            quantize_y(*GROUPS[-1], part)
